import numpy as np
import ml_dtypes


def mxq(x, axis, fmt="e4m3"):
    dtype, down = {"e4m3": (ml_dtypes.float8_e4m3fn, 7), "e5m2": (ml_dtypes.float8_e5m2, 14)}[fmt]
    v = np.moveaxis(np.asarray(x, np.float32).astype(ml_dtypes.bfloat16).astype(np.float64), axis, -1)
    blocks = v.reshape(v.shape[:-1] + (-1, 32))
    amax = np.abs(blocks).max(-1, keepdims=True)
    byte = np.maximum(np.where(amax > 0, np.frexp(amax)[1] - 1 + 127, 0) - down, 1)
    scale = np.exp2(byte - 127.0)
    codes = (blocks / scale).astype(np.float32).astype(dtype).astype(np.float64)
    return np.moveaxis((codes * scale).reshape(v.shape), -1, axis)


WIDE = False


def mx_kscale(k):
    if not WIDE:
        return np.ones(k)
    levels = np.array([10, -10, 5, -5, 0])
    if k % 512:
        return np.exp2(np.random.permutation(np.resize(levels, k // 32))).repeat(32)
    a = np.empty((k // 512, 16))
    for p in range(k // 512):
        a[p, :8] = np.random.permutation(np.resize(levels, 8))
        for g in range(8):
            far = levels[np.abs(levels - a[p, g]) >= 10]
            a[p, g + 8] = far[np.random.randint(len(far))]
    return np.exp2(a.ravel()).repeat(32)


def f64(x):
    return np.asarray(x).astype(np.float64)


def striped(idx):
    return np.tile(idx.reshape(-1, 16).T, (8, 1)).astype(np.uint16)


def unstriped(offs):
    return offs[:16].T.reshape(-1).astype(np.int64)


def pack_weight(w):
    k, n = w.shape
    w = f64(np.asarray(w, np.float32).astype(ml_dtypes.bfloat16)).reshape(k // 32, 32, n)
    amax = np.abs(w).max(1)
    byte = np.clip(np.where(amax > 0, np.frexp(amax)[1] - 1 + 127 - 7, 1), 1, 254)
    scaled = (w * np.exp2(127.0 - byte)[:, None, :]).reshape(k, n).astype(np.float32)
    words = np.ascontiguousarray(scaled.reshape(k // 512, 128, 4, n).transpose(0, 1, 3, 2)).astype(ml_dtypes.float8_e4m3fn).view(np.uint8)
    return words, np.ascontiguousarray(byte.astype(np.uint8).reshape(k // 512, 16, n))


def unpack_weight(words, scales):
    g, p, n, _ = words.shape
    vals = np.ascontiguousarray(words).view(ml_dtypes.float8_e4m3fn).astype(np.float64) * np.repeat(np.exp2(scales.astype(np.float64) - 127.0), 8, axis=1)[..., None]
    return vals.transpose(0, 1, 3, 2).reshape(g * 512, n)


def sigmoid(v):
    return 1.0 / (1.0 + np.exp(-np.maximum(v, -700.0)))


K, T, S, N, D = 1024, 1024, 512, 256, 2
P = 2 ** 7


def setup_inputs():
    n = np.random.standard_normal
    s = mx_kscale(K)[:, None]
    packed_xT = pack_weight(n((K, T)) * s)
    return {
        "x_words": packed_xT[0],
        "x_scales": packed_xT[1],
        "w1": (n((K, N)) / np.sqrt(K) / s).astype(np.float32),
        "gate": (np.tile(np.random.uniform(0.3, 0.6, (D, 1, S)), (1, P, 1))).astype(np.float32),
        "goal": ((np.random.uniform(size=(N, S)) < 0.3) * 1.0).astype(np.float32),
        "known": (np.tile((np.random.uniform(size=S) < 0.5) * 1.0, (P, 1))).astype(np.float32),
        "offs": striped(np.random.permutation(T)[:S]),
        "pos1": striped(np.random.permutation(S)[:S]),
        "pos2": striped(np.random.permutation(S)[:S]),
    }


def reference(x_words, x_scales, w1, gate, goal, known, offs, pos1, pos2):
    xq = unpack_weight(x_words, x_scales)[:, unstriped(offs)]
    p = sigmoid(mxq(f64(w1), 0, "e4m3").T @ xq)
    ee = (f64(goal) - p) * f64(known)[:1]
    ss = ee[:, unstriped(pos1)] * f64(gate)[0, :1] + ee[:, unstriped(pos2)] * f64(gate)[1, :1]
    return p + 0.7 * ss

@@ -1,0 +1,196 @@
+from contextlib import ExitStack
+
+import concourse.mybir as mybir
+from concourse.masks import make_identity
+
+K, T, S, N = 1024, 1024, 512, 256
+FLOPS = 2 * K * S * N
+
+F32 = mybir.dt.float32
+BF16 = mybir.dt.bfloat16
+I32 = mybir.dt.int32
+U32 = mybir.dt.uint32
+U16 = mybir.dt.uint16
+U8 = mybir.dt.uint8
+FP8X4 = mybir.dt.float8_e4m3fn_x4
+ACT = mybir.ActivationFunctionType
+ALU = mybir.AluOpType
+
+P = 128
+PACK = 4
+PASSES = K // (P * PACK)
+HALF = S // 2
+SPARE = 8
+SMOOTH = 0.7
+
+
+def tile_picked_ycns_one_p_kernel(tc, x_words, x_scales, w1, gate, goal, known, offs, pos1, pos2, out):
+    nc = tc.nc
+    with ExitStack() as ctx:
+        sb = ctx.enter_context(tc.tile_pool(name="sb", bufs=1))
+        ps = ctx.enter_context(tc.psum_pool(name="ps", bufs=1))
+
+        offs_t = sb.tile([P, S // 16], U16, name="offs_t")
+        pos_t = [sb.tile([P, S // 16], U16, name=f"pos_t{d}") for d in range(2)]
+        xs = sb.tile([P, T], U8, name="xs", align_bytes=64)
+        xw = [sb.tile([P, T], U32, name=f"xw{o}", align_bytes=64) for o in range(PASSES)]
+        wraw = [sb.tile([P, PACK, N], F32, name=f"wraw{o}") for o in range(PASSES)]
+        goal_t = [sb.tile([P, S], F32, name=f"goal_t{b}") for b in range(2)]
+        known_c = sb.tile([P, PACK], F32, name="known_c")
+        gate_b = [sb.tile([P, S], F32, name=f"gate_b{d}") for d in range(2)]
+        ident = sb.tile([P, P], F32, name="ident")
+        zeros = sb.tile([P, SPARE], F32, name="zeros")
+        ee = [sb.tile([P, S + SPARE], F32, name=f"ee{b}") for b in range(2)]
+
+        nc.vector.memset(xs[:].bitcast(I32), 0)
+        nc.vector.memset(zeros[:], 0.0)
+        nc.sync.dma_start(offs_t[:], offs)
+        for b in range(2):
+            nc.scalar.activation(ee[b][:, S:], zeros[:], ACT.Sigmoid)
+        make_identity(nc, ident[:])
+
+        def load_words(o):
+            nc.sync.dma_start(xw[o][:].bitcast(I32), x_words[o].rearrange("p n t -> p (n t)").bitcast(I32))
+
+        def load_w(o):
+            nc.sync.dma_start(wraw[o][:], w1[o * P * PACK : (o + 1) * P * PACK, :].rearrange("(p j) c -> p j c", j=PACK))
+
+        load_words(0)
+        for q in range(4):
+            nc.sync.dma_start(xs[32 * q : 32 * q + 8, :].bitcast(I32), x_scales[:, 4 * q : 4 * q + 4, :].bitcast(I32))
+        nc.sync.dma_start(known_c[:], known[0].rearrange("(p t) -> p t", t=PACK))
+        load_w(0)
+        load_w(1)
+        load_words(1)
+        nc.sync.dma_start(goal_t[0][:], goal[0:P, :])
+        nc.sync.dma_start(pos_t[0][:], pos1)
+        nc.sync.dma_start(gate_b[0][:], gate[0])
+        nc.sync.dma_start(goal_t[1][:], goal[P : 2 * P, :])
+        nc.sync.dma_start(pos_t[1][:], pos2)
+        nc.sync.dma_start(gate_b[1][:], gate[1])
+
+        def spread(bank, col):
+            for t in range(PACK):
+                nc.tensor.transpose(bank[:, t, :], col[:, t : t + 1].to_broadcast([P, P]), ident[:])
+
+        kbank = ps.tile([P, PACK, P], F32, name="kbank")
+        spread(kbank, known_c[:])
+        known_v = kbank[:].rearrange("p t n -> p n t")
+
+        xsg = sb.tile([P, S], U8, name="xsg", align_bytes=64)
+        xg = [sb.tile([P, S], U32, name="xg0", align_bytes=64)]
+        nc.vector.tensor_copy(xsg[:], xs[:].indirect(offs_t[:]))
+        nc.vector.tensor_copy(xg[0][:], xw[0][:].indirect(offs_t[:]))
+        wq, wsc = [], []
+        for o in range(PASSES):
+            grouped = sb.tile([P, N, PACK], BF16, name=f"grouped{o}", tag=f"grouped{o}", align_bytes=64)
+            split = N if o == 0 else N // 2
+            nc.scalar.copy(grouped[:, :split, :].rearrange("p (c i) t -> p c t i", i=4), wraw[o][:, :, :split].rearrange("p t (c i) -> p c t i", i=4))
+            if split < N:
+                nc.vector.tensor_copy(grouped[:, split:, :].rearrange("p (c i) t -> p c t i", i=4), wraw[o][:, :, split:].rearrange("p t (c i) -> p c t i", i=4))
+            codes = sb.tile([P, N], U32, name=f"wq{o}", align_bytes=64)
+            scales = sb.tile([P, N], U8, name=f"wsc{o}", align_bytes=64)
+            nc.vector.quantize_mx(out=codes[:].bitcast(FP8X4), scales=scales[:], in_=grouped[:].rearrange("p c t -> p (c t)"))
+            wq.append(codes)
+            wsc.append(scales)
+        halves = [slice(0, HALF), slice(HALF, S)]
+        quarters = [slice(q * P, (q + 1) * P) for q in range(4)]
+        xg.append(sb.tile([P, S], U32, name="xg1", tag="grouped1", align_bytes=64))
+        for cols in quarters:
+            nc.vector.tensor_copy(xg[1][:, cols], xw[1][:].indirect(offs_t[:, cols.start // 16 : cols.stop // 16]))
+
+        def mm(acc, b, cols, o):
+            rows = slice(b * P, (b + 1) * P)
+            nc.tensor.matmul_mx(
+                out=acc,
+                lhsT=wq[o][:, rows].bitcast(FP8X4),
+                lhsT_scale=wsc[o][:, rows],
+                rhs=xg[o][:, cols].bitcast(FP8X4),
+                rhs_scale=xsg[4 * o :, cols],
+                start=(o == 0),
+                stop=(o == PASSES - 1),
+            )
+
+        acc0 = [ps.tile([P, P], F32, name=f"acc0{q}", tag=f"acc0{q}") for q in range(4)]
+        acc1 = ps.tile([P, S], F32, name="acc1")
+        for o in range(PASSES):
+            for q in range(4):
+                mm(acc0[q][:], 0, quarters[q], o)
+            mm(acc1[:], 1, slice(0, S), o)
+
+        prob = [sb.tile([P, S], F32, name=f"prob{b}") for b in range(2)]
+        for q in range(4):
+            nc.scalar.activation(prob[0][:, quarters[q]], acc0[q][:], ACT.Sigmoid)
+        nc.scalar.activation(prob[1][:], acc1[:], ACT.Sigmoid)
+
+        diff = [sb.tile([P, S], F32, name=f"diff{b}") for b in range(2)]
+
+        def sub(b, cols):
+            nc.vector.tensor_tensor(diff[b][:, cols], goal_t[b][:, cols], prob[b][:, cols], ALU.subtract)
+
+        def mask(b, cols):
+            groups = slice(cols.start // PACK, cols.stop // PACK)
+            nc.vector.scalar_tensor_tensor(
+                ee[b][:, cols].rearrange("p (n t) -> p n t", t=PACK),
+                diff[b][:, cols].rearrange("p (n t) -> p n t", t=PACK),
+                SMOOTH,
+                known_v[:, groups, :],
+                ALU.mult,
+                ALU.mult,
+            )
+
+        term = [[sb.tile([P, S], F32, name=f"term{b}{d}") for d in range(2)] for b in range(2)]
+
+        def fetch(b, d, cols):
+            entries = slice(cols.start // 16, cols.stop // 16)
+            nc.vector.tensor_tensor(term[b][d][:, cols], ee[b][:].indirect(pos_t[d][:, entries]), gate_b[d][:, cols], ALU.mult)
+
+        whole = slice(0, S)
+        for h in range(2):
+            sub(0, quarters[2 * h])
+            sub(0, quarters[2 * h + 1])
+            mask(0, quarters[2 * h])
+            mask(0, quarters[2 * h + 1])
+        fetch(0, 0, whole)
+        sub(1, whole)
+        fetch(0, 1, halves[0])
+        mask(1, whole)
+        fetch(0, 1, halves[1])
+
+        def pe_sum(b, cols, tag_a, tag_b):
+            width = cols.stop - cols.start
+            turned = ps.tile([P, width], F32, name=f"turned{b}{cols.start}", tag=tag_a)
+            srcs = [prob[b], term[b][0], term[b][1]]
+            nq = width // P
+            for i, src in enumerate(srcs):
+                for q in range(nq):
+                    nc.tensor.matmul(
+                        turned[:, q * P : (q + 1) * P],
+                        src[:, cols.start + q * P : cols.start + (q + 1) * P],
+                        ident[:],
+                        is_transpose=True,
+                        start=(i == 0 and q == 0),
+                        stop=(i == len(srcs) - 1 and q == nq - 1),
+                    )
+            staged = sb.tile([P, width], F32, name=f"staged{b}{cols.start}")
+            nc.scalar.copy(staged[:], turned[:])
+            back = ps.tile([P, width], F32, name=f"back{b}{cols.start}", tag=tag_b)
+            for q in range(nq):
+                nc.tensor.transpose(back[:, q * P : (q + 1) * P], staged[:, q * P : (q + 1) * P], ident[:])
+            result = sb.tile([P, width], F32, name=f"result{b}{cols.start}")
+            nc.scalar.copy(result[:], back[:])
+            nc.sync.dma_start(out[b * P : (b + 1) * P, cols], result[:])
+
+        pe_sum(0, halves[0], "spare0", "acc00")
+        pe_sum(0, halves[1], "spare1", "acc01")
+        first, rest = slice(0, P), slice(P, S)
+        fetch(1, 0, first)
+        fetch(1, 1, first)
+        pe_sum(1, first, "acc02", "acc03")
+        fetch(1, 0, rest)
+        fetch(1, 1, rest)
+        part = sb.tile([P, S - P], F32, name="part")
+        last = sb.tile([P, S - P], F32, name="last")
+        nc.vector.tensor_tensor(part[:], term[1][0][:, rest], prob[1][:, rest], ALU.add)
+        nc.vector.tensor_tensor(last[:], part[:], term[1][1][:, rest], ALU.add)
+        nc.sync.dma_start(out[P : 2 * P, rest], last[:])

@@ -1,7 +1,6 @@
 from contextlib import ExitStack
 
 import concourse.mybir as mybir
-from concourse.masks import make_identity
 
 K, T, S, N = 1024, 1024, 512, 256
 FLOPS = 2 * K * S * N
@@ -26,6 +25,14 @@ SMOOTH = 0.7
 
 def tile_picked_ycns_one_p_kernel(tc, x_words, x_scales, w1, gate, goal, known, offs, pos1, pos2, out):
     nc = tc.nc
+    whole = slice(0, S)
+    halves = [slice(0, HALF), slice(HALF, S)]
+    quarters = [slice(q * P, (q + 1) * P) for q in range(4)]
+    blocks = [slice(0, P), slice(P, N)]
+
+    def entries(cols):
+        return slice(cols.start // 16, cols.stop // 16)
+
     with ExitStack() as ctx:
         sb = ctx.enter_context(tc.tile_pool(name="sb", bufs=1))
         ps = ctx.enter_context(tc.psum_pool(name="ps", bufs=1))
@@ -34,163 +41,187 @@ def tile_picked_ycns_one_p_kernel(tc, x_words, x_scales, w1, gate, goal, known, 
         pos_t = [sb.tile([P, S // 16], U16, name=f"pos_t{d}") for d in range(2)]
         xs = sb.tile([P, T], U8, name="xs", align_bytes=64)
         xw = [sb.tile([P, T], U32, name=f"xw{o}", align_bytes=64) for o in range(PASSES)]
-        wraw = [sb.tile([P, PACK, N], F32, name=f"wraw{o}") for o in range(PASSES)]
         goal_t = [sb.tile([P, S], F32, name=f"goal_t{b}") for b in range(2)]
-        known_c = sb.tile([P, PACK], F32, name="known_c")
-        gate_b = [sb.tile([P, S], F32, name=f"gate_b{d}") for d in range(2)]
+        gate_t = sb.tile([P, 2, S], F32, name="gate_t")
+        known_rows = sb.tile([P, P], F32, name="known_rows")
         ident = sb.tile([P, P], F32, name="ident")
         zeros = sb.tile([P, SPARE], F32, name="zeros")
-        ee = [sb.tile([P, S + SPARE], F32, name=f"ee{b}") for b in range(2)]
-
-        nc.vector.memset(xs[:].bitcast(I32), 0)
-        nc.vector.memset(zeros[:], 0.0)
-        nc.sync.dma_start(offs_t[:], offs)
-        for b in range(2):
-            nc.scalar.activation(ee[b][:, S:], zeros[:], ACT.Sigmoid)
-        make_identity(nc, ident[:])
+        ee0 = sb.tile([P, S + SPARE], F32, name="ee0")
+        ee1 = sb.tile([P, S], F32, name="ee1")
+        ee = [ee0, ee1]
 
         def load_words(o):
             nc.sync.dma_start(xw[o][:].bitcast(I32), x_words[o].rearrange("p n t -> p (n t)").bitcast(I32))
 
-        def load_w(o):
-            nc.sync.dma_start(wraw[o][:], w1[o * P * PACK : (o + 1) * P * PACK, :].rearrange("(p j) c -> p j c", j=PACK))
+        def load_w(o, cols):
+            raw = sb.tile([P, PACK, cols.stop - cols.start], F32, name=f"wraw{o}_{cols.start}", tag=f"wraw{o}_{cols.start}", align_bytes=64)
+            nc.sync.dma_start(raw[:], w1[o * P * PACK : (o + 1) * P * PACK, cols].rearrange("(p j) c -> p j c", j=PACK))
+            return raw
 
+        nc.vector.memset(xs[:].bitcast(I32), 0)
+        nc.vector.memset(zeros[:], 0.0)
+        nc.scalar.activation(ee0[:, S:], zeros[:], ACT.Sigmoid)
+        nc.vector.memset(known_rows[:], 0.0)
+        ones = sb.tile([P, 32], F32, name="ones")
+        ramp = sb.tile([P, 32], F32, name="ramp", align_bytes=64)
+        ramp_turned = sb.tile([P, 32], F32, name="ramp_turned", align_bytes=64)
+        nc.vector.memset(ones[:], 1.0)
+        nc.vector.memset(ident[:], 0.0)
+        nc.vector.tensor_tensor_scan(ramp[:], ones[:], ones[:], 0.0, ALU.mult, ALU.add)
+        nc.vector.transpose(ramp_turned[:], ramp[:])
+        for q in range(4):
+            rows = slice(32 * q, 32 * q + 32)
+            nc.vector.tensor_tensor(ident[rows, rows], ramp[rows, :], ramp_turned[rows, :], ALU.is_equal)
+        nc.sync.dma_start(offs_t[:], offs)
         load_words(0)
         for q in range(4):
             nc.sync.dma_start(xs[32 * q : 32 * q + 8, :].bitcast(I32), x_scales[:, 4 * q : 4 * q + 4, :].bitcast(I32))
-        nc.sync.dma_start(known_c[:], known[0].rearrange("(p t) -> p t", t=PACK))
-        load_w(0)
-        load_w(1)
+        nc.sync.dma_start(known_rows[0:4, :], known[0].rearrange("(c n) -> c n", n=P))
+        raw_pass0 = load_w(0, slice(0, N))
+        raw_pass1_block0 = load_w(1, blocks[0])
         load_words(1)
-        nc.sync.dma_start(goal_t[0][:], goal[0:P, :])
+        raw_pass1_block1 = load_w(1, blocks[1])
+        nc.sync.dma_start(goal_t[0][:], goal[blocks[0], :])
+        nc.sync.dma_start(goal_t[1][:], goal[blocks[1], :])
         nc.sync.dma_start(pos_t[0][:], pos1)
-        nc.sync.dma_start(gate_b[0][:], gate[0])
-        nc.sync.dma_start(goal_t[1][:], goal[P : 2 * P, :])
         nc.sync.dma_start(pos_t[1][:], pos2)
-        nc.sync.dma_start(gate_b[1][:], gate[1])
+        nc.sync.dma_start(gate_t[:], gate.rearrange("d p s -> p d s"))
 
-        def spread(bank, col):
-            for t in range(PACK):
-                nc.tensor.transpose(bank[:, t, :], col[:, t : t + 1].to_broadcast([P, P]), ident[:])
-
-        kbank = ps.tile([P, PACK, P], F32, name="kbank")
-        spread(kbank, known_c[:])
-        known_v = kbank[:].rearrange("p t n -> p n t")
+        known_turned = ps.tile([P, P], F32, name="known_turned", tag="bank7")
+        nc.tensor.transpose(known_turned[:], known_rows[:], ident[:])
+        weight = sb.tile([P, 4], F32, name="weight")
+        minus_weight = sb.tile([P, 4], F32, name="minus_weight")
+        nc.scalar.activation(weight[:], known_turned[:, 0:4], ACT.Copy, scale=SMOOTH)
+        nc.scalar.activation(minus_weight[:], known_turned[:, 0:4], ACT.Copy, scale=-SMOOTH)
+        weight_rows = ps.tile([P, S], F32, name="weight_rows", tag="bank6")
+        for q, cols in enumerate(quarters):
+            nc.tensor.transpose(weight_rows[:, cols], weight[:, q : q + 1].to_broadcast([P, P]), ident[:])
 
         xsg = sb.tile([P, S], U8, name="xsg", align_bytes=64)
-        xg = [sb.tile([P, S], U32, name="xg0", align_bytes=64)]
+        xg = [sb.tile([P, S], U32, name=f"xg{o}", align_bytes=64) for o in range(PASSES)]
+        wq = [sb.tile([P, PASSES, P], U32, name=f"wq{b}", align_bytes=64) for b in range(2)]
+        wsc = [sb.tile([P, PASSES, P], U8, name=f"wsc{b}", align_bytes=64) for b in range(2)]
+
+        def interleave(grouped, raw):
+            nc.scalar.copy(grouped.rearrange("p (c i) t -> p c t i", i=4), raw.rearrange("p t (c i) -> p c t i", i=4))
+
+        def gather_words(o, cols):
+            nc.vector.tensor_copy(xg[o][:, cols], xw[o][:].indirect(offs_t[:, entries(cols)]))
+
+        def quantize_block1(o, raw, tag):
+            grouped = sb.tile([P, P, PACK], BF16, name=f"grouped1{o}", tag=tag, align_bytes=64)
+            interleave(grouped[:], raw)
+            nc.vector.quantize_mx(out=wq[1][:, o].bitcast(FP8X4), scales=wsc[1][:, o], in_=grouped[:].rearrange("p c t -> p (c t)"))
+
+        gather_words(0, whole)
         nc.vector.tensor_copy(xsg[:], xs[:].indirect(offs_t[:]))
-        nc.vector.tensor_copy(xg[0][:], xw[0][:].indirect(offs_t[:]))
-        wq, wsc = [], []
-        for o in range(PASSES):
-            grouped = sb.tile([P, N, PACK], BF16, name=f"grouped{o}", tag=f"grouped{o}", align_bytes=64)
-            split = N if o == 0 else N // 2
-            nc.scalar.copy(grouped[:, :split, :].rearrange("p (c i) t -> p c t i", i=4), wraw[o][:, :, :split].rearrange("p t (c i) -> p c t i", i=4))
-            if split < N:
-                nc.vector.tensor_copy(grouped[:, split:, :].rearrange("p (c i) t -> p c t i", i=4), wraw[o][:, :, split:].rearrange("p t (c i) -> p c t i", i=4))
-            codes = sb.tile([P, N], U32, name=f"wq{o}", align_bytes=64)
-            scales = sb.tile([P, N], U8, name=f"wsc{o}", align_bytes=64)
-            nc.vector.quantize_mx(out=codes[:].bitcast(FP8X4), scales=scales[:], in_=grouped[:].rearrange("p c t -> p (c t)"))
-            wq.append(codes)
-            wsc.append(scales)
-        halves = [slice(0, HALF), slice(HALF, S)]
-        quarters = [slice(q * P, (q + 1) * P) for q in range(4)]
-        xg.append(sb.tile([P, S], U32, name="xg1", tag="grouped1", align_bytes=64))
-        for cols in quarters:
-            nc.vector.tensor_copy(xg[1][:, cols], xw[1][:].indirect(offs_t[:, cols.start // 16 : cols.stop // 16]))
+        grouped0 = sb.tile([P, PASSES, P, PACK], BF16, name="grouped0", align_bytes=64)
+        interleave(grouped0[:, 0], raw_pass0[:, :, blocks[0]])
+        interleave(grouped0[:, 1], raw_pass1_block0[:])
+        nc.vector.quantize_mx(
+            out=wq[0][:].rearrange("p o c -> p (o c)").bitcast(FP8X4),
+            scales=wsc[0][:].rearrange("p o c -> p (o c)"),
+            in_=grouped0[:].rearrange("p o c t -> p (o c t)"),
+        )
+        gather_words(1, quarters[0])
+        gather_words(1, quarters[1])
+        quantize_block1(0, raw_pass0[:, :, blocks[1]], "wraw1_0")
+        gather_words(1, quarters[2])
+        gather_words(1, quarters[3])
+        quantize_block1(1, raw_pass1_block1[:], "grouped11")
 
-        def mm(acc, b, cols, o):
-            rows = slice(b * P, (b + 1) * P)
-            nc.tensor.matmul_mx(
-                out=acc,
-                lhsT=wq[o][:, rows].bitcast(FP8X4),
-                lhsT_scale=wsc[o][:, rows],
-                rhs=xg[o][:, cols].bitcast(FP8X4),
-                rhs_scale=xsg[4 * o :, cols],
-                start=(o == 0),
-                stop=(o == PASSES - 1),
-            )
+        pieces = [(0, cols) for cols in quarters] + [(1, cols) for cols in halves]
+        acc = [ps.tile([P, cols.stop - cols.start], F32, name=f"acc{i}", tag=f"bank{i}") for i, (b, cols) in enumerate(pieces)]
+        order = [(i, o) for o in range(PASSES) for i in range(4)] + [(i, o) for o in range(PASSES) for i in (4, 5)]
+        for i, o in order:
+            for b, cols in pieces[i : i + 1]:
+                nc.tensor.matmul_mx(
+                    out=acc[i][:],
+                    lhsT=wq[b][:, o].bitcast(FP8X4),
+                    lhsT_scale=wsc[b][:, o],
+                    rhs=xg[o][:, cols].bitcast(FP8X4),
+                    rhs_scale=xsg[4 * o :, cols],
+                    start=(o == 0),
+                    stop=(o == PASSES - 1),
+                )
 
-        acc0 = [ps.tile([P, P], F32, name=f"acc0{q}", tag=f"acc0{q}") for q in range(4)]
-        acc1 = ps.tile([P, S], F32, name="acc1")
-        for o in range(PASSES):
-            for q in range(4):
-                mm(acc0[q][:], 0, quarters[q], o)
-            mm(acc1[:], 1, slice(0, S), o)
+        prob0 = sb.tile([P, S], F32, name="prob0")
+        for q, cols in enumerate(quarters):
+            nc.scalar.activation(prob0[:, cols], acc[q][:], ACT.Sigmoid)
+        rest1 = sb.tile([P, S], F32, name="rest1")
+        for h, cols in enumerate(halves):
+            nc.scalar.activation(rest1[:, cols], acc[4 + h][:], ACT.Sigmoid, scale=-1.0)
+        prob = [prob0, rest1]
 
-        prob = [sb.tile([P, S], F32, name=f"prob{b}") for b in range(2)]
-        for q in range(4):
-            nc.scalar.activation(prob[0][:, quarters[q]], acc0[q][:], ACT.Sigmoid)
-        nc.scalar.activation(prob[1][:], acc1[:], ACT.Sigmoid)
+        diff = sb.tile([P, S], F32, name="diff")
+        for pair in (quarters[:2], quarters[2:]):
+            for cols in pair:
+                nc.vector.tensor_tensor(diff[:, cols], goal_t[0][:, cols], prob0[:, cols], ALU.subtract)
+            for cols in pair:
+                nc.vector.tensor_tensor(ee0[:, cols], diff[:, cols], weight_rows[:, cols], ALU.mult)
 
-        diff = [sb.tile([P, S], F32, name=f"diff{b}") for b in range(2)]
+        def turn(bank, sources, cols):
+            width = cols.stop - cols.start
+            for i, source in enumerate(sources):
+                for c in range(0, width, P):
+                    nc.tensor.matmul(
+                        bank[:, c : c + P],
+                        source[:, cols.start + c : cols.start + c + P],
+                        ident[:],
+                        is_transpose=True,
+                        start=(i == 0 and c == 0),
+                        stop=(i == len(sources) - 1 and c == width - P),
+                    )
 
-        def sub(b, cols):
-            nc.vector.tensor_tensor(diff[b][:, cols], goal_t[b][:, cols], prob[b][:, cols], ALU.subtract)
-
-        def mask(b, cols):
-            groups = slice(cols.start // PACK, cols.stop // PACK)
-            nc.vector.scalar_tensor_tensor(
-                ee[b][:, cols].rearrange("p (n t) -> p n t", t=PACK),
-                diff[b][:, cols].rearrange("p (n t) -> p n t", t=PACK),
-                SMOOTH,
-                known_v[:, groups, :],
-                ALU.mult,
-                ALU.mult,
-            )
+        ee1_turned = sb.tile([P, S], F32, name="ee1_turned")
+        for h, cols in enumerate(halves):
+            sums = ps.tile([P, HALF], F32, name=f"sums{h}", tag=("bank7", "bank0")[h])
+            turn(sums, [goal_t[1], rest1], cols)
+            for c in range(2):
+                q = 2 * h + c
+                nc.scalar.activation(
+                    ee1_turned[:, quarters[q]], sums[:, c * P : (c + 1) * P], ACT.Identity, scale=minus_weight[:, q : q + 1], bias=weight[:, q : q + 1]
+                )
+        for h, cols in enumerate(halves):
+            upright = ps.tile([P, HALF], F32, name=f"upright{h}", tag=f"bank{1 + h}")
+            turn(upright, [ee1_turned], cols)
+            nc.scalar.copy(ee1[:, cols], upright[:])
 
         term = [[sb.tile([P, S], F32, name=f"term{b}{d}") for d in range(2)] for b in range(2)]
 
         def fetch(b, d, cols):
-            entries = slice(cols.start // 16, cols.stop // 16)
-            nc.vector.tensor_tensor(term[b][d][:, cols], ee[b][:].indirect(pos_t[d][:, entries]), gate_b[d][:, cols], ALU.mult)
+            nc.vector.tensor_tensor(term[b][d][:, cols], ee[b][:].indirect(pos_t[d][:, entries(cols)]), gate_t[:, d, cols], ALU.mult)
 
-        whole = slice(0, S)
-        for h in range(2):
-            sub(0, quarters[2 * h])
-            sub(0, quarters[2 * h + 1])
-            mask(0, quarters[2 * h])
-            mask(0, quarters[2 * h + 1])
-        fetch(0, 0, whole)
-        sub(1, whole)
-        fetch(0, 1, halves[0])
-        mask(1, whole)
-        fetch(0, 1, halves[1])
-
-        def pe_sum(b, cols, tag_a, tag_b):
+        def sum_on_tensor(b, cols, tag_turned, tag_back):
             width = cols.stop - cols.start
-            turned = ps.tile([P, width], F32, name=f"turned{b}{cols.start}", tag=tag_a)
-            srcs = [prob[b], term[b][0], term[b][1]]
-            nq = width // P
-            for i, src in enumerate(srcs):
-                for q in range(nq):
-                    nc.tensor.matmul(
-                        turned[:, q * P : (q + 1) * P],
-                        src[:, cols.start + q * P : cols.start + (q + 1) * P],
-                        ident[:],
-                        is_transpose=True,
-                        start=(i == 0 and q == 0),
-                        stop=(i == len(srcs) - 1 and q == nq - 1),
-                    )
-            staged = sb.tile([P, width], F32, name=f"staged{b}{cols.start}")
+            turned = ps.tile([P, width], F32, name=f"turned{b}_{cols.start}", tag=tag_turned)
+            turn(turned, [term[b][0], prob[b], term[b][1]], cols)
+            staged = sb.tile([P, width], F32, name=f"staged{b}_{cols.start}")
             nc.scalar.copy(staged[:], turned[:])
-            back = ps.tile([P, width], F32, name=f"back{b}{cols.start}", tag=tag_b)
-            for q in range(nq):
-                nc.tensor.transpose(back[:, q * P : (q + 1) * P], staged[:, q * P : (q + 1) * P], ident[:])
-            result = sb.tile([P, width], F32, name=f"result{b}{cols.start}")
-            nc.scalar.copy(result[:], back[:])
-            nc.sync.dma_start(out[b * P : (b + 1) * P, cols], result[:])
+            back = ps.tile([P, width], F32, name=f"back{b}_{cols.start}", tag=tag_back)
+            turn(back, [staged], slice(0, width))
+            result = sb.tile([P, width], F32, name=f"result{b}_{cols.start}")
+            if b == 0:
+                nc.scalar.copy(result[:], back[:])
+            else:
+                nc.scalar.activation(result[:], back[:], ACT.Copy, scale=-1.0, bias=1.0)
+            nc.scalar.dma_start(out[blocks[b], cols], result[:])
 
-        pe_sum(0, halves[0], "spare0", "acc00")
-        pe_sum(0, halves[1], "spare1", "acc01")
-        first, rest = slice(0, P), slice(P, S)
+        fetch(0, 0, whole)
+        fetch(0, 1, halves[0])
+        sum_on_tensor(0, halves[0], "bank3", "bank5")
+        fetch(0, 1, halves[1])
+        sum_on_tensor(0, halves[1], "bank4", "bank6")
+        first, rest, middle, last = quarters[0], slice(P, S), slice(P, S - P), quarters[3]
         fetch(1, 0, first)
         fetch(1, 1, first)
-        pe_sum(1, first, "acc02", "acc03")
+        sum_on_tensor(1, first, "bank7", "bank0")
+        part = sb.tile([P, S], F32, name="part")
+        final = sb.tile([P, S], F32, name="final")
         fetch(1, 0, rest)
-        fetch(1, 1, rest)
-        part = sb.tile([P, S - P], F32, name="part")
-        last = sb.tile([P, S - P], F32, name="last")
-        nc.vector.tensor_tensor(part[:], term[1][0][:, rest], prob[1][:, rest], ALU.add)
-        nc.vector.tensor_tensor(last[:], part[:], term[1][1][:, rest], ALU.add)
-        nc.sync.dma_start(out[P : 2 * P, rest], last[:])
+        fetch(1, 1, middle)
+        nc.vector.scalar_tensor_tensor(part[:, rest], rest1[:, rest], 1.0, term[1][0][:, rest], ALU.subtract, ALU.add)
+        fetch(1, 1, last)
+        for cols in (middle, last):
+            nc.vector.scalar_tensor_tensor(final[:, cols], part[:, cols], -1.0, term[1][1][:, cols], ALU.mult, ALU.subtract)
+            nc.sync.dma_start(out[blocks[1], cols], final[:, cols])

@@ -16,149 +16,148 @@ ACT = mybir.ActivationFunctionType
 ALU = mybir.AluOpType
 
 P = 128
+QUADRANT = 32
 PACK = 4
 PASSES = K // (P * PACK)
-HALF = S // 2
-SPARE = 8
+PER_COLUMN = 16
 SMOOTH = 0.7
 
 
 def tile_picked_ycns_one_p_kernel(tc, x_words, x_scales, w1, gate, goal, known, offs, pos1, pos2, out):
     nc = tc.nc
-    whole = slice(0, S)
-    halves = [slice(0, HALF), slice(HALF, S)]
-    quarters = [slice(q * P, (q + 1) * P) for q in range(4)]
     blocks = [slice(0, P), slice(P, N)]
+    halves = [slice(0, S // 2), slice(S // 2, S)]
+    quarters = [slice(q * P, (q + 1) * P) for q in range(S // P)]
 
     def entries(cols):
-        return slice(cols.start // 16, cols.stop // 16)
+        return slice(cols.start // PER_COLUMN, cols.stop // PER_COLUMN)
 
     with ExitStack() as ctx:
         sb = ctx.enter_context(tc.tile_pool(name="sb", bufs=1))
         ps = ctx.enter_context(tc.psum_pool(name="ps", bufs=1))
 
-        offs_t = sb.tile([P, S // 16], U16, name="offs_t")
-        pos_t = [sb.tile([P, S // 16], U16, name=f"pos_t{d}") for d in range(2)]
-        xs = sb.tile([P, T], U8, name="xs", align_bytes=64)
-        xw = [sb.tile([P, T], U32, name=f"xw{o}", align_bytes=64) for o in range(PASSES)]
+        offs_t = sb.tile([P, S // PER_COLUMN], U16, name="offs_t")
+        pos_t = [sb.tile([P, S // PER_COLUMN], U16, name=f"pos_t{d}") for d in range(2)]
+        scale_table = sb.tile([P, T], U8, name="scale_table", align_bytes=64)
+        word_table = [sb.tile([P, T], U32, name=f"word_table{o}", align_bytes=64) for o in range(PASSES)]
         goal_t = [sb.tile([P, S], F32, name=f"goal_t{b}") for b in range(2)]
         gate_t = sb.tile([P, 2, S], F32, name="gate_t")
-        known_rows = sb.tile([P, P], F32, name="known_rows")
+        known_t = sb.tile([P, PACK], F32, name="known_t")
+
+        nc.vector.memset(scale_table[:].bitcast(I32), 0)
+
         ident = sb.tile([P, P], F32, name="ident")
-        zeros = sb.tile([P, SPARE], F32, name="zeros")
-        ee0 = sb.tile([P, S + SPARE], F32, name="ee0")
-        ee1 = sb.tile([P, S], F32, name="ee1")
-        ee = [ee0, ee1]
-
-        def load_words(o):
-            nc.sync.dma_start(xw[o][:].bitcast(I32), x_words[o].rearrange("p n t -> p (n t)").bitcast(I32))
-
-        def load_w(o, cols):
-            raw = sb.tile([P, PACK, cols.stop - cols.start], F32, name=f"wraw{o}_{cols.start}", tag=f"wraw{o}_{cols.start}", align_bytes=64)
-            nc.sync.dma_start(raw[:], w1[o * P * PACK : (o + 1) * P * PACK, cols].rearrange("(p j) c -> p j c", j=PACK))
-            return raw
-
-        nc.vector.memset(xs[:].bitcast(I32), 0)
-        nc.vector.memset(zeros[:], 0.0)
-        nc.scalar.activation(ee0[:, S:], zeros[:], ACT.Sigmoid)
-        nc.vector.memset(known_rows[:], 0.0)
-        ones = sb.tile([P, 32], F32, name="ones")
-        ramp = sb.tile([P, 32], F32, name="ramp", align_bytes=64)
-        ramp_turned = sb.tile([P, 32], F32, name="ramp_turned", align_bytes=64)
+        ones = sb.tile([P, QUADRANT], F32, name="ones")
+        step = sb.tile([P, QUADRANT], F32, name="step")
+        ramp = sb.tile([P, QUADRANT], F32, name="ramp", align_bytes=64)
+        ramp_turned = sb.tile([P, QUADRANT], F32, name="ramp_turned", align_bytes=64)
         nc.vector.memset(ones[:], 1.0)
         nc.vector.memset(ident[:], 0.0)
-        nc.vector.tensor_tensor_scan(ramp[:], ones[:], ones[:], 0.0, ALU.mult, ALU.add)
+        nc.scalar.activation(step[:], ones[:], ACT.Sigmoid)
+        nc.vector.tensor_tensor_scan(ramp[:], ones[:], step[:], 0.0, ALU.mult, ALU.add)
         nc.vector.transpose(ramp_turned[:], ramp[:])
-        for q in range(4):
-            rows = slice(32 * q, 32 * q + 32)
+        for q in range(P // QUADRANT):
+            rows = slice(QUADRANT * q, QUADRANT * (q + 1))
             nc.vector.tensor_tensor(ident[rows, rows], ramp[rows, :], ramp_turned[rows, :], ALU.is_equal)
+
+        def load_words(o):
+            nc.sync.dma_start(word_table[o][:].bitcast(I32), x_words[o].rearrange("p n t -> p (n t)").bitcast(I32))
+
+        def load_w(o, labels):
+            raw = sb.tile([P, PACK, labels.stop - labels.start], F32, name=f"w_raw{o}_{labels.start}")
+            nc.sync.dma_start(raw[:], w1[o * P * PACK : (o + 1) * P * PACK, labels].rearrange("(p t) c -> p t c", t=PACK))
+            return raw
+
         nc.sync.dma_start(offs_t[:], offs)
         load_words(0)
-        for q in range(4):
-            nc.sync.dma_start(xs[32 * q : 32 * q + 8, :].bitcast(I32), x_scales[:, 4 * q : 4 * q + 4, :].bitcast(I32))
-        nc.sync.dma_start(known_rows[0:4, :], known[0].rearrange("(c n) -> c n", n=P))
-        raw_pass0 = load_w(0, slice(0, N))
-        raw_pass1_block0 = load_w(1, blocks[0])
+        for q in range(P // QUADRANT):
+            live = slice(QUADRANT * q, QUADRANT * q + PASSES * PACK)
+            nc.sync.dma_start(scale_table[live, :].bitcast(I32), x_scales[:, PACK * q : PACK * (q + 1), :].bitcast(I32))
+        nc.sync.dma_start(known_t[:], known[0].rearrange("(n t) -> n t", t=PACK))
+        w_pass0 = load_w(0, slice(0, N))
+        w_pass1_block0 = load_w(1, blocks[0])
         load_words(1)
-        raw_pass1_block1 = load_w(1, blocks[1])
+        w_pass1_block1 = load_w(1, blocks[1])
         nc.sync.dma_start(goal_t[0][:], goal[blocks[0], :])
-        nc.sync.dma_start(goal_t[1][:], goal[blocks[1], :])
         nc.sync.dma_start(pos_t[0][:], pos1)
         nc.sync.dma_start(pos_t[1][:], pos2)
+        nc.sync.dma_start(goal_t[1][:], goal[blocks[1], :])
         nc.sync.dma_start(gate_t[:], gate.rearrange("d p s -> p d s"))
 
-        known_turned = ps.tile([P, P], F32, name="known_turned", tag="bank7")
-        nc.tensor.transpose(known_turned[:], known_rows[:], ident[:])
-        weight = sb.tile([P, 4], F32, name="weight")
-        minus_weight = sb.tile([P, 4], F32, name="minus_weight")
-        nc.scalar.activation(weight[:], known_turned[:, 0:4], ACT.Copy, scale=SMOOTH)
-        nc.scalar.activation(minus_weight[:], known_turned[:, 0:4], ACT.Copy, scale=-SMOOTH)
-        weight_rows = ps.tile([P, S], F32, name="weight_rows", tag="bank6")
-        for q, cols in enumerate(quarters):
-            nc.tensor.transpose(weight_rows[:, cols], weight[:, q : q + 1].to_broadcast([P, P]), ident[:])
+        known_bank = ps.tile([P, PACK, P], F32, name="known_bank")
+        for t in range(PACK):
+            nc.tensor.transpose(known_bank[:, t, :], known_t[:, t : t + 1].to_broadcast([P, P]), ident[:])
+        known_rows = known_bank[:].rearrange("p t n -> p n t")
 
-        xsg = sb.tile([P, S], U8, name="xsg", align_bytes=64)
-        xg = [sb.tile([P, S], U32, name=f"xg{o}", align_bytes=64) for o in range(PASSES)]
-        wq = [sb.tile([P, PASSES, P], U32, name=f"wq{b}", align_bytes=64) for b in range(2)]
-        wsc = [sb.tile([P, PASSES, P], U8, name=f"wsc{b}", align_bytes=64) for b in range(2)]
+        x_scales_picked = sb.tile([P, S], U8, name="x_scales_picked", align_bytes=64)
+        x_words_picked = [sb.tile([P, S], U32, name=f"x_words_picked{o}", align_bytes=64) for o in range(PASSES)]
+        w_words = [sb.tile([P, N], U32, name=f"w_words{o}", align_bytes=64) for o in range(PASSES)]
+        w_scales = [sb.tile([P, N], U8, name=f"w_scales{o}", align_bytes=64) for o in range(PASSES)]
 
-        def interleave(grouped, raw):
-            nc.scalar.copy(grouped.rearrange("p (c i) t -> p c t i", i=4), raw.rearrange("p t (c i) -> p c t i", i=4))
+        def quantize(raw, o, labels):
+            grouped = sb.tile([P, labels.stop - labels.start, PACK], BF16, name=f"grouped{o}_{labels.start}", align_bytes=64)
+            nc.scalar.copy(grouped[:].rearrange("p (c i) t -> p c t i", i=4), raw[:].rearrange("p t (c i) -> p c t i", i=4))
+            nc.vector.quantize_mx(
+                out=w_words[o][:, labels].bitcast(FP8X4), scales=w_scales[o][:, labels], in_=grouped[:].rearrange("p c t -> p (c t)")
+            )
 
         def gather_words(o, cols):
-            nc.vector.tensor_copy(xg[o][:, cols], xw[o][:].indirect(offs_t[:, entries(cols)]))
+            nc.vector.tensor_copy(x_words_picked[o][:, cols], word_table[o][:].indirect(offs_t[:, entries(cols)]))
 
-        def quantize_block1(o, raw, tag):
-            grouped = sb.tile([P, P, PACK], BF16, name=f"grouped1{o}", tag=tag, align_bytes=64)
-            interleave(grouped[:], raw)
-            nc.vector.quantize_mx(out=wq[1][:, o].bitcast(FP8X4), scales=wsc[1][:, o], in_=grouped[:].rearrange("p c t -> p (c t)"))
+        pieces = [(0, halves[0]), (0, quarters[2]), (0, quarters[3]), (1, halves[0]), (1, halves[1])]
 
-        gather_words(0, whole)
-        nc.vector.tensor_copy(xsg[:], xs[:].indirect(offs_t[:]))
-        grouped0 = sb.tile([P, PASSES, P, PACK], BF16, name="grouped0", align_bytes=64)
-        interleave(grouped0[:, 0], raw_pass0[:, :, blocks[0]])
-        interleave(grouped0[:, 1], raw_pass1_block0[:])
-        nc.vector.quantize_mx(
-            out=wq[0][:].rearrange("p o c -> p (o c)").bitcast(FP8X4),
-            scales=wsc[0][:].rearrange("p o c -> p (o c)"),
-            in_=grouped0[:].rearrange("p o c t -> p (o c t)"),
-        )
-        gather_words(1, quarters[0])
-        gather_words(1, quarters[1])
-        quantize_block1(0, raw_pass0[:, :, blocks[1]], "wraw1_0")
-        gather_words(1, quarters[2])
-        gather_words(1, quarters[3])
-        quantize_block1(1, raw_pass1_block1[:], "grouped11")
+        gather_words(0, slice(0, S))
+        nc.vector.tensor_copy(x_scales_picked[:], scale_table[:].indirect(offs_t[:]))
+        quantize(w_pass0, 0, slice(0, N))
+        quantize(w_pass1_block0, 1, blocks[0])
+        for b, cols in pieces:
+            if b == 0:
+                gather_words(1, cols)
+        quantize(w_pass1_block1, 1, blocks[1])
 
-        pieces = [(0, cols) for cols in quarters] + [(1, cols) for cols in halves]
-        acc = [ps.tile([P, cols.stop - cols.start], F32, name=f"acc{i}", tag=f"bank{i}") for i, (b, cols) in enumerate(pieces)]
-        order = [(i, o) for o in range(PASSES) for i in range(4)] + [(i, o) for o in range(PASSES) for i in (4, 5)]
-        for i, o in order:
-            for b, cols in pieces[i : i + 1]:
+        logits = [ps.tile([P, cols.stop - cols.start], F32, name=f"logits{i}", tag=f"bank{i}") for i, (b, cols) in enumerate(pieces)]
+        for o in range(PASSES):
+            for i, (b, cols) in enumerate(pieces):
                 nc.tensor.matmul_mx(
-                    out=acc[i][:],
-                    lhsT=wq[b][:, o].bitcast(FP8X4),
-                    lhsT_scale=wsc[b][:, o],
-                    rhs=xg[o][:, cols].bitcast(FP8X4),
-                    rhs_scale=xsg[4 * o :, cols],
+                    out=logits[i][:],
+                    lhsT=w_words[o][:, blocks[b]].bitcast(FP8X4),
+                    lhsT_scale=w_scales[o][:, blocks[b]],
+                    rhs=x_words_picked[o][:, cols].bitcast(FP8X4),
+                    rhs_scale=x_scales_picked[PACK * o :, cols],
                     start=(o == 0),
                     stop=(o == PASSES - 1),
                 )
 
-        prob0 = sb.tile([P, S], F32, name="prob0")
-        for q, cols in enumerate(quarters):
-            nc.scalar.activation(prob0[:, cols], acc[q][:], ACT.Sigmoid)
-        rest1 = sb.tile([P, S], F32, name="rest1")
-        for h, cols in enumerate(halves):
-            nc.scalar.activation(rest1[:, cols], acc[4 + h][:], ACT.Sigmoid, scale=-1.0)
-        prob = [prob0, rest1]
+        prob = [sb.tile([P, S], F32, name=f"prob{b}") for b in range(2)]
+        for i, (b, cols) in enumerate(pieces):
+            nc.scalar.activation(prob[b][:, cols], logits[i][:], ACT.Sigmoid)
 
-        diff = sb.tile([P, S], F32, name="diff")
-        for pair in (quarters[:2], quarters[2:]):
-            for cols in pair:
-                nc.vector.tensor_tensor(diff[:, cols], goal_t[0][:, cols], prob0[:, cols], ALU.subtract)
-            for cols in pair:
-                nc.vector.tensor_tensor(ee0[:, cols], diff[:, cols], weight_rows[:, cols], ALU.mult)
+        diff = [sb.tile([P, S], F32, name=f"diff{b}") for b in range(2)]
+        errors = [sb.tile([P, S], F32, name=f"errors{b}") for b in range(2)]
+
+        def subtract(b, cols):
+            nc.vector.tensor_tensor(diff[b][:, cols], goal_t[b][:, cols], prob[b][:, cols], ALU.subtract)
+
+        def mask(b, cols):
+            nc.vector.scalar_tensor_tensor(
+                errors[b][:, cols].rearrange("p (n t) -> p n t", t=PACK),
+                diff[b][:, cols].rearrange("p (n t) -> p n t", t=PACK),
+                SMOOTH,
+                known_rows[:, cols.start // PACK : cols.stop // PACK, :],
+                ALU.mult,
+                ALU.mult,
+            )
+
+        subtract(*pieces[0])
+        for piece, following in zip(pieces, pieces[1:]):
+            subtract(*following)
+            mask(*piece)
+        mask(*pieces[-1])
+
+        term = [[sb.tile([P, S], F32, name=f"term{b}{d}") for d in range(2)] for b in range(2)]
+
+        def fetch(b, d, cols):
+            nc.vector.tensor_tensor(term[b][d][:, cols], errors[b][:].indirect(pos_t[d][:, entries(cols)]), gate_t[:, d, cols], ALU.mult)
 
         def turn(bank, sources, cols):
             width = cols.stop - cols.start
@@ -173,55 +172,31 @@ def tile_picked_ycns_one_p_kernel(tc, x_words, x_scales, w1, gate, goal, known, 
                         stop=(i == len(sources) - 1 and c == width - P),
                     )
 
-        ee1_turned = sb.tile([P, S], F32, name="ee1_turned")
-        for h, cols in enumerate(halves):
-            sums = ps.tile([P, HALF], F32, name=f"sums{h}", tag=("bank7", "bank0")[h])
-            turn(sums, [goal_t[1], rest1], cols)
-            for c in range(2):
-                q = 2 * h + c
-                nc.scalar.activation(
-                    ee1_turned[:, quarters[q]], sums[:, c * P : (c + 1) * P], ACT.Identity, scale=minus_weight[:, q : q + 1], bias=weight[:, q : q + 1]
-                )
-        for h, cols in enumerate(halves):
-            upright = ps.tile([P, HALF], F32, name=f"upright{h}", tag=f"bank{1 + h}")
-            turn(upright, [ee1_turned], cols)
-            nc.scalar.copy(ee1[:, cols], upright[:])
-
-        term = [[sb.tile([P, S], F32, name=f"term{b}{d}") for d in range(2)] for b in range(2)]
-
-        def fetch(b, d, cols):
-            nc.vector.tensor_tensor(term[b][d][:, cols], ee[b][:].indirect(pos_t[d][:, entries(cols)]), gate_t[:, d, cols], ALU.mult)
-
-        def sum_on_tensor(b, cols, tag_turned, tag_back):
+        def finish_on_tensor(b, cols, turned_tag, back_tag):
             width = cols.stop - cols.start
-            turned = ps.tile([P, width], F32, name=f"turned{b}_{cols.start}", tag=tag_turned)
-            turn(turned, [term[b][0], prob[b], term[b][1]], cols)
+            fetch(b, 0, cols)
+            fetch(b, 1, cols)
+            turned = ps.tile([P, width], F32, name=f"turned{b}_{cols.start}", tag=turned_tag)
+            turn(turned, [prob[b], term[b][0], term[b][1]], cols)
             staged = sb.tile([P, width], F32, name=f"staged{b}_{cols.start}")
             nc.scalar.copy(staged[:], turned[:])
-            back = ps.tile([P, width], F32, name=f"back{b}_{cols.start}", tag=tag_back)
+            back = ps.tile([P, width], F32, name=f"back{b}_{cols.start}", tag=back_tag)
             turn(back, [staged], slice(0, width))
             result = sb.tile([P, width], F32, name=f"result{b}_{cols.start}")
-            if b == 0:
-                nc.scalar.copy(result[:], back[:])
-            else:
-                nc.scalar.activation(result[:], back[:], ACT.Copy, scale=-1.0, bias=1.0)
+            nc.scalar.copy(result[:], back[:])
             nc.scalar.dma_start(out[blocks[b], cols], result[:])
 
-        fetch(0, 0, whole)
-        fetch(0, 1, halves[0])
-        sum_on_tensor(0, halves[0], "bank3", "bank5")
-        fetch(0, 1, halves[1])
-        sum_on_tensor(0, halves[1], "bank4", "bank6")
-        first, rest, middle, last = quarters[0], slice(P, S), slice(P, S - P), quarters[3]
-        fetch(1, 0, first)
-        fetch(1, 1, first)
-        sum_on_tensor(1, first, "bank7", "bank0")
+        finish_on_tensor(0, halves[0], "bank3", "bank0")
+        finish_on_tensor(0, halves[1], "bank4", "bank1")
+        finish_on_tensor(1, quarters[0], "bank5", "bank2")
+
+        rest, middle, last = slice(P, S), slice(P, S - P), quarters[-1]
         part = sb.tile([P, S], F32, name="part")
         final = sb.tile([P, S], F32, name="final")
         fetch(1, 0, rest)
         fetch(1, 1, middle)
-        nc.vector.scalar_tensor_tensor(part[:, rest], rest1[:, rest], 1.0, term[1][0][:, rest], ALU.subtract, ALU.add)
+        nc.vector.tensor_tensor(part[:, rest], term[1][0][:, rest], prob[1][:, rest], ALU.add)
         fetch(1, 1, last)
         for cols in (middle, last):
-            nc.vector.scalar_tensor_tensor(final[:, cols], part[:, cols], -1.0, term[1][1][:, cols], ALU.mult, ALU.subtract)
+            nc.vector.tensor_tensor(final[:, cols], part[:, cols], term[1][1][:, cols], ALU.add)
             nc.sync.dma_start(out[blocks[1], cols], final[:, cols])

@@ -1,6 +1,7 @@
 from contextlib import ExitStack
 
 import concourse.mybir as mybir
+from concourse.masks import make_identity
 
 K, T, S, N = 1024, 1024, 512, 256
 FLOPS = 2 * K * S * N
@@ -20,6 +21,7 @@ QUADRANT = 32
 PACK = 4
 PASSES = K // (P * PACK)
 PER_COLUMN = 16
+SPARE = 8
 SMOOTH = 0.7
 
 
@@ -41,24 +43,17 @@ def tile_picked_ycns_one_p_kernel(tc, x_words, x_scales, w1, gate, goal, known, 
         scale_table = sb.tile([P, T], U8, name="scale_table", align_bytes=64)
         word_table = [sb.tile([P, T], U32, name=f"word_table{o}", align_bytes=64) for o in range(PASSES)]
         goal_t = [sb.tile([P, S], F32, name=f"goal_t{b}") for b in range(2)]
-        gate_t = sb.tile([P, 2, S], F32, name="gate_t")
+        gate_t = [sb.tile([P, S], F32, name=f"gate_t{d}") for d in range(2)]
         known_t = sb.tile([P, PACK], F32, name="known_t")
 
         nc.vector.memset(scale_table[:].bitcast(I32), 0)
 
+        errors = [sb.tile([P, S + SPARE], F32, name="errors0"), sb.tile([P, S], F32, name="errors1")]
+        zeros = sb.tile([P, SPARE], F32, name="zeros")
+        nc.vector.memset(zeros[:], 0.0)
+        nc.scalar.activation(errors[0][:, S:], zeros[:], ACT.Sigmoid)
         ident = sb.tile([P, P], F32, name="ident")
-        ones = sb.tile([P, QUADRANT], F32, name="ones")
-        step = sb.tile([P, QUADRANT], F32, name="step")
-        ramp = sb.tile([P, QUADRANT], F32, name="ramp", align_bytes=64)
-        ramp_turned = sb.tile([P, QUADRANT], F32, name="ramp_turned", align_bytes=64)
-        nc.vector.memset(ones[:], 1.0)
-        nc.vector.memset(ident[:], 0.0)
-        nc.scalar.activation(step[:], ones[:], ACT.Sigmoid)
-        nc.vector.tensor_tensor_scan(ramp[:], ones[:], step[:], 0.0, ALU.mult, ALU.add)
-        nc.vector.transpose(ramp_turned[:], ramp[:])
-        for q in range(P // QUADRANT):
-            rows = slice(QUADRANT * q, QUADRANT * (q + 1))
-            nc.vector.tensor_tensor(ident[rows, rows], ramp[rows, :], ramp_turned[rows, :], ALU.is_equal)
+        make_identity(nc, ident[:])
 
         def load_words(o):
             nc.sync.dma_start(word_table[o][:].bitcast(I32), x_words[o].rearrange("p n t -> p (n t)").bitcast(I32))
@@ -82,12 +77,12 @@ def tile_picked_ycns_one_p_kernel(tc, x_words, x_scales, w1, gate, goal, known, 
         nc.sync.dma_start(pos_t[0][:], pos1)
         nc.sync.dma_start(pos_t[1][:], pos2)
         nc.sync.dma_start(goal_t[1][:], goal[blocks[1], :])
-        nc.sync.dma_start(gate_t[:], gate.rearrange("d p s -> p d s"))
+        nc.sync.dma_start(gate_t[0][:], gate[0])
+        nc.sync.dma_start(gate_t[1][:], gate[1])
 
-        known_bank = ps.tile([P, PACK, P], F32, name="known_bank")
+        known_rows = ps.tile([P, S], F32, name="known_rows")
         for t in range(PACK):
-            nc.tensor.transpose(known_bank[:, t, :], known_t[:, t : t + 1].to_broadcast([P, P]), ident[:])
-        known_rows = known_bank[:].rearrange("p t n -> p n t")
+            nc.tensor.transpose(known_rows[:, t:S:PACK], known_t[:, t : t + 1].to_broadcast([P, P]), ident[:])
 
         x_scales_picked = sb.tile([P, S], U8, name="x_scales_picked", align_bytes=64)
         x_words_picked = [sb.tile([P, S], U32, name=f"x_words_picked{o}", align_bytes=64) for o in range(PASSES)]
@@ -133,20 +128,12 @@ def tile_picked_ycns_one_p_kernel(tc, x_words, x_scales, w1, gate, goal, known, 
             nc.scalar.activation(prob[b][:, cols], logits[i][:], ACT.Sigmoid)
 
         diff = [sb.tile([P, S], F32, name=f"diff{b}") for b in range(2)]
-        errors = [sb.tile([P, S], F32, name=f"errors{b}") for b in range(2)]
 
         def subtract(b, cols):
             nc.vector.tensor_tensor(diff[b][:, cols], goal_t[b][:, cols], prob[b][:, cols], ALU.subtract)
 
         def mask(b, cols):
-            nc.vector.scalar_tensor_tensor(
-                errors[b][:, cols].rearrange("p (n t) -> p n t", t=PACK),
-                diff[b][:, cols].rearrange("p (n t) -> p n t", t=PACK),
-                SMOOTH,
-                known_rows[:, cols.start // PACK : cols.stop // PACK, :],
-                ALU.mult,
-                ALU.mult,
-            )
+            nc.vector.scalar_tensor_tensor(errors[b][:, cols], diff[b][:, cols], SMOOTH, known_rows[:, cols], ALU.mult, ALU.mult)
 
         subtract(*pieces[0])
         for piece, following in zip(pieces, pieces[1:]):
@@ -157,7 +144,7 @@ def tile_picked_ycns_one_p_kernel(tc, x_words, x_scales, w1, gate, goal, known, 
         term = [[sb.tile([P, S], F32, name=f"term{b}{d}") for d in range(2)] for b in range(2)]
 
         def fetch(b, d, cols):
-            nc.vector.tensor_tensor(term[b][d][:, cols], errors[b][:].indirect(pos_t[d][:, entries(cols)]), gate_t[:, d, cols], ALU.mult)
+            nc.vector.tensor_tensor(term[b][d][:, cols], errors[b][:].indirect(pos_t[d][:, entries(cols)]), gate_t[d][:, cols], ALU.mult)
 
         def turn(bank, sources, cols):
             width = cols.stop - cols.start
@@ -174,8 +161,6 @@ def tile_picked_ycns_one_p_kernel(tc, x_words, x_scales, w1, gate, goal, known, 
 
         def finish_on_tensor(b, cols, turned_tag, back_tag):
             width = cols.stop - cols.start
-            fetch(b, 0, cols)
-            fetch(b, 1, cols)
             turned = ps.tile([P, width], F32, name=f"turned{b}_{cols.start}", tag=turned_tag)
             turn(turned, [prob[b], term[b][0], term[b][1]], cols)
             staged = sb.tile([P, width], F32, name=f"staged{b}_{cols.start}")
@@ -184,10 +169,15 @@ def tile_picked_ycns_one_p_kernel(tc, x_words, x_scales, w1, gate, goal, known, 
             turn(back, [staged], slice(0, width))
             result = sb.tile([P, width], F32, name=f"result{b}_{cols.start}")
             nc.scalar.copy(result[:], back[:])
-            nc.scalar.dma_start(out[blocks[b], cols], result[:])
+            nc.sync.dma_start(out[blocks[b], cols], result[:])
 
+        fetch(0, 0, slice(0, S))
+        fetch(0, 1, halves[0])
         finish_on_tensor(0, halves[0], "bank3", "bank0")
+        fetch(0, 1, halves[1])
         finish_on_tensor(0, halves[1], "bank4", "bank1")
+        fetch(1, 0, quarters[0])
+        fetch(1, 1, quarters[0])
         finish_on_tensor(1, quarters[0], "bank5", "bank2")
 
         rest, middle, last = slice(P, S), slice(P, S - P), quarters[-1]

@@ -86,44 +86,52 @@ def tile_picked_ycns_one_p_kernel(tc, x_words, x_scales, w1, gate, goal, known, 
 
         x_scales_picked = sb.tile([P, S], U8, name="x_scales_picked", align_bytes=64)
         x_words_picked = [sb.tile([P, S], U32, name=f"x_words_picked{o}", align_bytes=64) for o in range(PASSES)]
-        w_words = [sb.tile([P, N], U32, name=f"w_words{o}", align_bytes=64) for o in range(PASSES)]
-        w_scales = [sb.tile([P, N], U8, name=f"w_scales{o}", align_bytes=64) for o in range(PASSES)]
+        w_words = [sb.tile([P, PASSES * P], U32, name=f"w_words{b}", align_bytes=64) for b in range(2)]
+        w_scales = [sb.tile([P, PASSES * P], U8, name=f"w_scales{b}", align_bytes=64) for b in range(2)]
 
-        def quantize(raw, o, labels):
-            grouped = sb.tile([P, labels.stop - labels.start, PACK], BF16, name=f"grouped{o}_{labels.start}", align_bytes=64)
-            nc.scalar.copy(grouped[:].rearrange("p (c i) t -> p c t i", i=4), raw[:].rearrange("p t (c i) -> p c t i", i=4))
-            nc.vector.quantize_mx(
-                out=w_words[o][:, labels].bitcast(FP8X4), scales=w_scales[o][:, labels], in_=grouped[:].rearrange("p c t -> p (c t)")
-            )
+        def interleave(dst, raw):
+            nc.scalar.copy(dst.rearrange("p (c i t) -> p c t i", i=4, t=PACK), raw.rearrange("p t (c i) -> p c t i", i=4))
+
+        def quantize(b, cols, grouped):
+            nc.vector.quantize_mx(out=w_words[b][:, cols].bitcast(FP8X4), scales=w_scales[b][:, cols], in_=grouped)
 
         def gather_words(o, cols):
             nc.vector.tensor_copy(x_words_picked[o][:, cols], word_table[o][:].indirect(offs_t[:, entries(cols)]))
 
-        pieces = [(0, halves[0]), (0, quarters[2]), (0, quarters[3]), (1, halves[0]), (1, halves[1])]
+        pieces = [(0, quarters[0]), (0, slice(P, 3 * P)), (0, quarters[3]), (1, halves[0]), (1, halves[1])]
 
         gather_words(0, slice(0, S))
         nc.vector.tensor_copy(x_scales_picked[:], scale_table[:].indirect(offs_t[:]))
-        quantize(w_pass0, 0, slice(0, N))
-        quantize(w_pass1_block0, 1, blocks[0])
+        grouped00 = sb.tile([P, P * PACK], BF16, name="grouped00", tag="grouped", align_bytes=64)
+        grouped01 = sb.tile([P, P * PACK], BF16, name="grouped01", align_bytes=64)
+        interleave(grouped00[:], w_pass0[:, :, blocks[0]])
+        interleave(grouped01[:], w_pass1_block0[:])
+        quantize(0, slice(0, P), grouped00[:])
+        quantize(0, slice(P, 2 * P), grouped01[:])
+        grouped1 = sb.tile([P, PASSES * P * PACK], BF16, name="grouped1", tag="grouped", align_bytes=64)
+        interleave(grouped1[:, : P * PACK], w_pass0[:, :, blocks[1]])
+        interleave(grouped1[:, P * PACK :], w_pass1_block1[:])
         for b, cols in pieces:
             if b == 0:
                 gather_words(1, cols)
-        quantize(w_pass1_block1, 1, blocks[1])
+        quantize(1, slice(0, 2 * P), grouped1[:])
 
         logits = [ps.tile([P, cols.stop - cols.start], F32, name=f"logits{i}", tag=f"bank{i}") for i, (b, cols) in enumerate(pieces)]
-        for o in range(PASSES):
+        for b_now, o in ((0, 0), (0, 1), (1, 0), (1, 1)):
             for i, (b, cols) in enumerate(pieces):
+                if b != b_now:
+                    continue
                 nc.tensor.matmul_mx(
                     out=logits[i][:],
-                    lhsT=w_words[o][:, blocks[b]].bitcast(FP8X4),
-                    lhsT_scale=w_scales[o][:, blocks[b]],
+                    lhsT=w_words[b][:, o * P : (o + 1) * P].bitcast(FP8X4),
+                    lhsT_scale=w_scales[b][:, o * P : (o + 1) * P],
                     rhs=x_words_picked[o][:, cols].bitcast(FP8X4),
                     rhs_scale=x_scales_picked[PACK * o :, cols],
                     start=(o == 0),
                     stop=(o == PASSES - 1),
                 )
 
-        prob = [sb.tile([P, S], F32, name=f"prob{b}") for b in range(2)]
+        prob = [sb.tile([P, S], F32, name="prob0", tag=f"w_raw1_{P}"), sb.tile([P, S], F32, name="prob1")]
         for i, (b, cols) in enumerate(pieces):
             nc.scalar.activation(prob[b][:, cols], logits[i][:], ACT.Sigmoid)
 
@@ -146,6 +154,14 @@ def tile_picked_ycns_one_p_kernel(tc, x_words, x_scales, w1, gate, goal, known, 
         def fetch(b, d, cols):
             nc.vector.tensor_tensor(term[b][d][:, cols], errors[b][:].indirect(pos_t[d][:, entries(cols)]), gate_t[d][:, cols], ALU.mult)
 
+        fetched = [[sb.tile([P, S], F32, name=f"fetched{b}{d}") for d in range(2)] for b in range(2)]
+
+        def fetch_plain(b, d, cols):
+            nc.scalar.activation(fetched[b][d][:, cols], errors[b][:].indirect(pos_t[d][:, entries(cols)]), ACT.Copy)
+
+        def weigh(b, d, cols):
+            nc.vector.tensor_tensor(term[b][d][:, cols], fetched[b][d][:, cols], gate_t[d][:, cols], ALU.mult)
+
         def turn(bank, sources, cols):
             width = cols.stop - cols.start
             for i, source in enumerate(sources):
@@ -159,34 +175,53 @@ def tile_picked_ycns_one_p_kernel(tc, x_words, x_scales, w1, gate, goal, known, 
                         stop=(i == len(sources) - 1 and c == width - P),
                     )
 
-        def finish_on_tensor(b, cols, turned_tag, back_tag):
+        def stage(b, cols, tag):
             width = cols.stop - cols.start
-            turned = ps.tile([P, width], F32, name=f"turned{b}_{cols.start}", tag=turned_tag)
+            turned = ps.tile([P, width], F32, name=f"turned{b}_{cols.start}", tag=tag)
             turn(turned, [prob[b], term[b][0], term[b][1]], cols)
             staged = sb.tile([P, width], F32, name=f"staged{b}_{cols.start}")
             nc.scalar.copy(staged[:], turned[:])
-            back = ps.tile([P, width], F32, name=f"back{b}_{cols.start}", tag=back_tag)
+            return staged
+
+        results = [sb.tile([P, S], F32, name=f"result{b}") for b in range(2)]
+
+        def finish(b, cols, staged, tag):
+            width = cols.stop - cols.start
+            back = ps.tile([P, width], F32, name=f"back{b}_{cols.start}", tag=tag)
             turn(back, [staged], slice(0, width))
-            result = sb.tile([P, width], F32, name=f"result{b}_{cols.start}")
-            nc.scalar.copy(result[:], back[:])
-            nc.sync.dma_start(out[blocks[b], cols], result[:])
+            nc.scalar.copy(results[b][:, cols], back[:])
 
-        fetch(0, 0, slice(0, S))
+        def store(b, cols):
+            nc.sync.dma_start(out[blocks[b], cols], results[b][:, cols])
+
+        for b in range(2):
+            for cols in halves:
+                fetch_plain(b, 0, cols)
         fetch(0, 1, halves[0])
-        finish_on_tensor(0, halves[0], "bank3", "bank0")
+        weigh(0, 0, halves[0])
+        staged_a = stage(0, halves[0], "bank3")
         fetch(0, 1, halves[1])
-        finish_on_tensor(0, halves[1], "bank4", "bank1")
-        fetch(1, 0, quarters[0])
+        weigh(0, 0, halves[1])
+        staged_b = stage(0, halves[1], "bank4")
         fetch(1, 1, quarters[0])
-        finish_on_tensor(1, quarters[0], "bank5", "bank2")
+        weigh(1, 0, halves[0])
+        staged_c = stage(1, quarters[0], "bank5")
+        fetch(1, 1, quarters[1])
+        staged_d = stage(1, quarters[1], "bank6")
+        finish(0, halves[0], staged_a, "bank0")
+        store(0, halves[0])
+        finish(0, halves[1], staged_b, "bank1")
+        store(0, halves[1])
+        finish(1, quarters[0], staged_c, "bank2")
+        finish(1, quarters[1], staged_d, "bank3")
+        store(1, halves[0])
 
-        rest, middle, last = slice(P, S), slice(P, S - P), quarters[-1]
         part = sb.tile([P, S], F32, name="part")
-        final = sb.tile([P, S], F32, name="final")
-        fetch(1, 0, rest)
-        fetch(1, 1, middle)
-        nc.vector.tensor_tensor(part[:, rest], term[1][0][:, rest], prob[1][:, rest], ALU.add)
-        fetch(1, 1, last)
-        for cols in (middle, last):
-            nc.vector.tensor_tensor(final[:, cols], part[:, cols], term[1][1][:, cols], ALU.add)
-            nc.sync.dma_start(out[blocks[1], cols], final[:, cols])
+        fetch(1, 1, quarters[2])
+        weigh(1, 0, halves[1])
+        fetch(1, 1, quarters[3])
+        nc.vector.tensor_tensor(part[:, halves[1]], term[1][0][:, halves[1]], prob[1][:, halves[1]], ALU.add)
+        final = sb.tile([P, S // 2], F32, name="final", tag="staged1_0")
+        for i, cols in enumerate(quarters[2:]):
+            nc.vector.tensor_tensor(final[:, quarters[i]], part[:, cols], term[1][1][:, cols], ALU.add)
+            nc.sync.dma_start(out[blocks[1], cols], final[:, quarters[i]])

@@ -194,34 +194,37 @@ def tile_picked_ycns_one_p_kernel(tc, x_words, x_scales, w1, gate, goal, known, 
         def store(b, cols):
             nc.sync.dma_start(out[blocks[b], cols], results[b][:, cols])
 
-        for b in range(2):
-            for cols in halves:
-                fetch_plain(b, 0, cols)
+        part = sb.tile([P, S], F32, name="part")
+
+        def add_first(cols):
+            nc.vector.tensor_tensor(part[:, cols], term[1][0][:, cols], prob[1][:, cols], ALU.add)
+
+        def add_second(cols):
+            nc.vector.tensor_tensor(results[1][:, cols], part[:, cols], term[1][1][:, cols], ALU.add)
+            store(1, cols)
+
+        fetch_plain(0, 0, halves[0])
+        fetch_plain(0, 0, halves[1])
+        fetch_plain(1, 0, halves[0])
+        fetch_plain(1, 1, halves[0])
+        fetch_plain(1, 0, halves[1])
         fetch(0, 1, halves[0])
         weigh(0, 0, halves[0])
         staged_a = stage(0, halves[0], "bank3")
         fetch(0, 1, halves[1])
         weigh(0, 0, halves[1])
         staged_b = stage(0, halves[1], "bank4")
-        fetch(1, 1, quarters[0])
-        weigh(1, 0, halves[0])
-        staged_c = stage(1, quarters[0], "bank5")
-        fetch(1, 1, quarters[1])
-        staged_d = stage(1, quarters[1], "bank6")
         finish(0, halves[0], staged_a, "bank0")
         store(0, halves[0])
         finish(0, halves[1], staged_b, "bank1")
         store(0, halves[1])
-        finish(1, quarters[0], staged_c, "bank2")
-        finish(1, quarters[1], staged_d, "bank3")
-        store(1, halves[0])
-
-        part = sb.tile([P, S], F32, name="part")
-        fetch(1, 1, quarters[2])
+        weigh(1, 0, halves[0])
+        weigh(1, 1, halves[0])
+        add_first(halves[0])
         weigh(1, 0, halves[1])
+        add_second(halves[0])
+        fetch(1, 1, quarters[2])
+        add_first(halves[1])
         fetch(1, 1, quarters[3])
-        nc.vector.tensor_tensor(part[:, halves[1]], term[1][0][:, halves[1]], prob[1][:, halves[1]], ALU.add)
-        final = sb.tile([P, S // 2], F32, name="final", tag="staged1_0")
-        for i, cols in enumerate(quarters[2:]):
-            nc.vector.tensor_tensor(final[:, quarters[i]], part[:, cols], term[1][1][:, cols], ALU.add)
-            nc.sync.dma_start(out[blocks[1], cols], final[:, quarters[i]])
+        add_second(quarters[2])
+        add_second(quarters[3])

@@ -203,11 +203,9 @@ def tile_picked_ycns_one_p_kernel(tc, x_words, x_scales, w1, gate, goal, known, 
             nc.vector.tensor_tensor(results[1][:, cols], part[:, cols], term[1][1][:, cols], ALU.add)
             store(1, cols)
 
-        fetch_plain(0, 0, halves[0])
-        fetch_plain(0, 0, halves[1])
-        fetch_plain(1, 0, halves[0])
-        fetch_plain(1, 1, halves[0])
-        fetch_plain(1, 0, halves[1])
+        for b in range(2):
+            for cols in halves:
+                fetch_plain(b, 0, cols)
         fetch(0, 1, halves[0])
         weigh(0, 0, halves[0])
         staged_a = stage(0, halves[0], "bank3")
@@ -219,7 +217,7 @@ def tile_picked_ycns_one_p_kernel(tc, x_words, x_scales, w1, gate, goal, known, 
         finish(0, halves[1], staged_b, "bank1")
         store(0, halves[1])
         weigh(1, 0, halves[0])
-        weigh(1, 1, halves[0])
+        fetch(1, 1, halves[0])
         add_first(halves[0])
         weigh(1, 0, halves[1])
         add_second(halves[0])

@@ -43,8 +43,9 @@ def tile_picked_ycns_one_p_kernel(tc, x_words, x_scales, w1, gate, goal, known, 
         scale_table = sb.tile([P, T], U8, name="scale_table", align_bytes=64)
         word_table = [sb.tile([P, T], U32, name=f"word_table{o}", align_bytes=64) for o in range(PASSES)]
         goal_t = [sb.tile([P, S], F32, name=f"goal_t{b}") for b in range(2)]
-        gate_t = [sb.tile([P, S], F32, name=f"gate_t{d}") for d in range(2)]
+        gate_t = sb.tile([P, 2, S], F32, name="gate_t")
         known_t = sb.tile([P, PACK], F32, name="known_t")
+        gate_runs = sb.tile([P, P], F32, name="gate_runs")
 
         nc.vector.memset(scale_table[:].bitcast(I32), 0)
 
@@ -52,6 +53,7 @@ def tile_picked_ycns_one_p_kernel(tc, x_words, x_scales, w1, gate, goal, known, 
         zeros = sb.tile([P, SPARE], F32, name="zeros")
         nc.vector.memset(zeros[:], 0.0)
         nc.scalar.activation(errors[0][:, S:], zeros[:], ACT.Sigmoid)
+        nc.gpsimd.memset(gate_runs[:], 0.0)
         ident = sb.tile([P, P], F32, name="ident")
         make_identity(nc, ident[:])
 
@@ -76,11 +78,11 @@ def tile_picked_ycns_one_p_kernel(tc, x_words, x_scales, w1, gate, goal, known, 
         nc.sync.dma_start(goal_t[0][:], goal[blocks[0], :])
         nc.sync.dma_start(pos_t[0][:], pos1)
         nc.sync.dma_start(pos_t[1][:], pos2)
+        nc.sync.dma_start(gate_runs[: 2 * len(quarters), :], gate[:, 0, :].rearrange("d (s n) -> d s n", n=P))
         nc.sync.dma_start(goal_t[1][:], goal[blocks[1], :])
-        nc.sync.dma_start(gate_t[0][:], gate[0])
-        nc.sync.dma_start(gate_t[1][:], gate[1])
+        nc.sync.dma_start(gate_t[:], gate.rearrange("d p n -> p d n"))
 
-        known_rows = ps.tile([P, S], F32, name="known_rows")
+        known_rows = ps.tile([P, S], F32, name="known_rows", tag="known_bank")
         for t in range(PACK):
             nc.tensor.transpose(known_rows[:, t:S:PACK], known_t[:, t : t + 1].to_broadcast([P, P]), ident[:])
 
@@ -117,19 +119,25 @@ def tile_picked_ycns_one_p_kernel(tc, x_words, x_scales, w1, gate, goal, known, 
         quantize(1, slice(0, 2 * P), grouped1[:])
 
         logits = [ps.tile([P, cols.stop - cols.start], F32, name=f"logits{i}", tag=f"bank{i}") for i, (b, cols) in enumerate(pieces)]
-        for b_now, o in ((0, 0), (0, 1), (1, 0), (1, 1)):
-            for i, (b, cols) in enumerate(pieces):
-                if b != b_now:
-                    continue
-                nc.tensor.matmul_mx(
-                    out=logits[i][:],
-                    lhsT=w_words[b][:, o * P : (o + 1) * P].bitcast(FP8X4),
-                    lhsT_scale=w_scales[b][:, o * P : (o + 1) * P],
-                    rhs=x_words_picked[o][:, cols].bitcast(FP8X4),
-                    rhs_scale=x_scales_picked[PACK * o :, cols],
-                    start=(o == 0),
-                    stop=(o == PASSES - 1),
-                )
+
+        def multiply(i, o):
+            b, cols = pieces[i]
+            nc.tensor.matmul_mx(
+                out=logits[i][:],
+                lhsT=w_words[b][:, o * P : (o + 1) * P].bitcast(FP8X4),
+                lhsT_scale=w_scales[b][:, o * P : (o + 1) * P],
+                rhs=x_words_picked[o][:, cols].bitcast(FP8X4),
+                rhs_scale=x_scales_picked[PACK * o :, cols],
+                start=(o == 0),
+                stop=(o == PASSES - 1),
+            )
+
+        for o in range(PASSES):
+            for i in range(3):
+                multiply(i, o)
+        for i in range(3, 5):
+            for o in range(PASSES):
+                multiply(i, o)
 
         prob = [sb.tile([P, S], F32, name="prob0", tag=f"w_raw1_{P}"), sb.tile([P, S], F32, name="prob1")]
         for i, (b, cols) in enumerate(pieces):
@@ -149,21 +157,37 @@ def tile_picked_ycns_one_p_kernel(tc, x_words, x_scales, w1, gate, goal, known, 
             mask(*piece)
         mask(*pieces[-1])
 
-        term = [[sb.tile([P, S], F32, name=f"term{b}{d}") for d in range(2)] for b in range(2)]
+        results = [sb.tile([P, S], F32, name=f"result{b}") for b in range(2)]
 
-        def fetch(b, d, cols):
-            nc.vector.tensor_tensor(term[b][d][:, cols], errors[b][:].indirect(pos_t[d][:, entries(cols)]), gate_t[d][:, cols], ALU.mult)
+        def store(b, cols):
+            nc.sync.dma_start(out[blocks[b], cols], results[b][:, cols])
 
-        fetched = [[sb.tile([P, S], F32, name=f"fetched{b}{d}") for d in range(2)] for b in range(2)]
+        gate_bank = ps.tile([P, P], F32, name="gate_bank", tag="bank5")
+        nc.tensor.transpose(gate_bank[:], gate_runs[:], ident[:])
+        gate_columns = sb.tile([P, 2 * len(quarters)], F32, name="gate_columns")
+        nc.scalar.copy(gate_columns[:], gate_bank[:, : 2 * len(quarters)])
 
-        def fetch_plain(b, d, cols):
-            nc.scalar.activation(fetched[b][d][:, cols], errors[b][:].indirect(pos_t[d][:, entries(cols)]), ACT.Copy)
+        fetched = [sb.tile([P, S], F32, name=f"fetched{d}") for d in range(2)]
+        prob_turned = sb.tile([P, S // 2], F32, name="prob_turned")
+        weighed = [sb.tile([P, S], F32, name=f"weighed{d}") for d in range(2)]
 
-        def weigh(b, d, cols):
-            nc.vector.tensor_tensor(term[b][d][:, cols], fetched[b][d][:, cols], gate_t[d][:, cols], ALU.mult)
+        def fetch_and_turn(d, cols, tag):
+            nc.scalar.activation(fetched[d][:, cols], errors[0][:].indirect(pos_t[d][:, entries(cols)]), ACT.Copy)
+            bank = ps.tile([P, cols.stop - cols.start], F32, name=f"turned{d}_{cols.start}", tag=tag)
+            for c in range(cols.start, cols.stop, P):
+                nc.tensor.transpose(bank[:, c - cols.start : c - cols.start + P], fetched[d][:, c : c + P], ident[:])
+            return bank
 
-        def turn(bank, sources, cols):
+        def weigh_turned(d, cols, bank):
+            for c in range(cols.start, cols.stop, P):
+                column = len(quarters) * d + c // P
+                nc.scalar.activation(
+                    weighed[d][:, c : c + P], bank[:, c - cols.start : c - cols.start + P], ACT.Copy, scale=gate_columns[:, column : column + 1]
+                )
+
+        def turn_back(sources, cols, tag):
             width = cols.stop - cols.start
+            bank = ps.tile([P, width], F32, name=f"back{cols.start}", tag=tag)
             for i, source in enumerate(sources):
                 for c in range(0, width, P):
                     nc.tensor.matmul(
@@ -174,55 +198,54 @@ def tile_picked_ycns_one_p_kernel(tc, x_words, x_scales, w1, gate, goal, known, 
                         start=(i == 0 and c == 0),
                         stop=(i == len(sources) - 1 and c == width - P),
                     )
+            return bank
 
-        def stage(b, cols, tag):
-            width = cols.stop - cols.start
-            turned = ps.tile([P, width], F32, name=f"turned{b}_{cols.start}", tag=tag)
-            turn(turned, [prob[b], term[b][0], term[b][1]], cols)
-            staged = sb.tile([P, width], F32, name=f"staged{b}_{cols.start}")
-            nc.scalar.copy(staged[:], turned[:])
-            return staged
+        def turn_prob(cols, tag):
+            bank = ps.tile([P, cols.stop - cols.start], F32, name=f"prob_bank{cols.start}", tag=tag)
+            for c in range(cols.start, cols.stop, P):
+                nc.tensor.transpose(bank[:, c - cols.start : c - cols.start + P], prob[0][:, c : c + P], ident[:])
+            nc.scalar.copy(prob_turned[:, cols], bank[:])
 
-        results = [sb.tile([P, S], F32, name=f"result{b}") for b in range(2)]
+        def copy_back(cols, bank):
+            nc.scalar.copy(results[0][:, cols], bank[:])
+            store(0, cols)
 
-        def finish(b, cols, staged, tag):
-            width = cols.stop - cols.start
-            back = ps.tile([P, width], F32, name=f"back{b}_{cols.start}", tag=tag)
-            turn(back, [staged], slice(0, width))
-            nc.scalar.copy(results[b][:, cols], back[:])
+        def add_back(cols, bank):
+            nc.vector.tensor_tensor(results[0][:, cols], prob[0][:, cols], bank[:], ALU.add)
+            store(0, cols)
 
-        def store(b, cols):
-            nc.sync.dma_start(out[blocks[b], cols], results[b][:, cols])
-
+        term = [sb.tile([P, S], F32, name=f"term{d}") for d in range(2)]
         part = sb.tile([P, S], F32, name="part")
 
+        def fetch(d, cols):
+            nc.vector.tensor_tensor(term[d][:, cols], errors[1][:].indirect(pos_t[d][:, entries(cols)]), gate_t[:, d, cols], ALU.mult)
+
         def add_first(cols):
-            nc.vector.tensor_tensor(part[:, cols], term[1][0][:, cols], prob[1][:, cols], ALU.add)
+            nc.vector.tensor_tensor(part[:, cols], term[0][:, cols], prob[1][:, cols], ALU.add)
 
         def add_second(cols):
-            nc.vector.tensor_tensor(results[1][:, cols], part[:, cols], term[1][1][:, cols], ALU.add)
+            nc.vector.tensor_tensor(results[1][:, cols], part[:, cols], term[1][:, cols], ALU.add)
             store(1, cols)
 
-        for b in range(2):
-            for cols in halves:
-                fetch_plain(b, 0, cols)
-        fetch(0, 1, halves[0])
-        weigh(0, 0, halves[0])
-        staged_a = stage(0, halves[0], "bank3")
-        fetch(0, 1, halves[1])
-        weigh(0, 0, halves[1])
-        staged_b = stage(0, halves[1], "bank4")
-        finish(0, halves[0], staged_a, "bank0")
-        store(0, halves[0])
-        finish(0, halves[1], staged_b, "bank1")
-        store(0, halves[1])
-        weigh(1, 0, halves[0])
-        fetch(1, 1, halves[0])
+        steps = [(0, halves[0], "bank0"), (1, halves[0], "bank1"), (0, halves[1], "bank2"), (1, halves[1], "bank5")]
+        turned = [fetch_and_turn(*step) for step in steps]
+        turn_prob(halves[0], "bank4")
+        for (d, cols, tag), bank in zip(steps, turned):
+            weigh_turned(d, cols, bank)
+        back_a = turn_back([prob_turned] + weighed, halves[0], "bank6")
+        back_b = turn_back(weighed, quarters[2], "bank3")
+        back_c = turn_back(weighed, quarters[3], "bank4")
+        copy_back(halves[0], back_a)
+
+        fetch(0, halves[0])
+        fetch(1, halves[0])
         add_first(halves[0])
-        weigh(1, 0, halves[1])
+        fetch(0, halves[1])
         add_second(halves[0])
-        fetch(1, 1, quarters[2])
         add_first(halves[1])
-        fetch(1, 1, quarters[3])
+        fetch(1, quarters[2])
+        fetch(1, quarters[3])
         add_second(quarters[2])
         add_second(quarters[3])
+        add_back(quarters[2], back_b)
+        add_back(quarters[3], back_c)

@@ -168,7 +168,6 @@ def tile_picked_ycns_one_p_kernel(tc, x_words, x_scales, w1, gate, goal, known, 
         nc.scalar.copy(gate_columns[:], gate_bank[:, : 2 * len(quarters)])
 
         fetched = [sb.tile([P, S], F32, name=f"fetched{d}") for d in range(2)]
-        prob_turned = sb.tile([P, S // 2], F32, name="prob_turned")
         weighed = [sb.tile([P, S], F32, name=f"weighed{d}") for d in range(2)]
 
         def fetch_and_turn(d, cols, tag):
@@ -185,30 +184,20 @@ def tile_picked_ycns_one_p_kernel(tc, x_words, x_scales, w1, gate, goal, known, 
                     weighed[d][:, c : c + P], bank[:, c - cols.start : c - cols.start + P], ACT.Copy, scale=gate_columns[:, column : column + 1]
                 )
 
-        def turn_back(sources, cols, tag):
+        def turn_back(cols, tag):
             width = cols.stop - cols.start
             bank = ps.tile([P, width], F32, name=f"back{cols.start}", tag=tag)
-            for i, source in enumerate(sources):
+            for d in range(2):
                 for c in range(0, width, P):
                     nc.tensor.matmul(
                         bank[:, c : c + P],
-                        source[:, cols.start + c : cols.start + c + P],
+                        weighed[d][:, cols.start + c : cols.start + c + P],
                         ident[:],
                         is_transpose=True,
-                        start=(i == 0 and c == 0),
-                        stop=(i == len(sources) - 1 and c == width - P),
+                        start=(d == 0 and c == 0),
+                        stop=(d == 1 and c == width - P),
                     )
             return bank
-
-        def turn_prob(cols, tag):
-            bank = ps.tile([P, cols.stop - cols.start], F32, name=f"prob_bank{cols.start}", tag=tag)
-            for c in range(cols.start, cols.stop, P):
-                nc.tensor.transpose(bank[:, c - cols.start : c - cols.start + P], prob[0][:, c : c + P], ident[:])
-            nc.scalar.copy(prob_turned[:, cols], bank[:])
-
-        def copy_back(cols, bank):
-            nc.scalar.copy(results[0][:, cols], bank[:])
-            store(0, cols)
 
         def add_back(cols, bank):
             nc.vector.tensor_tensor(results[0][:, cols], prob[0][:, cols], bank[:], ALU.add)
@@ -229,13 +218,11 @@ def tile_picked_ycns_one_p_kernel(tc, x_words, x_scales, w1, gate, goal, known, 
 
         steps = [(0, halves[0], "bank0"), (1, halves[0], "bank1"), (0, halves[1], "bank2"), (1, halves[1], "bank5")]
         turned = [fetch_and_turn(*step) for step in steps]
-        turn_prob(halves[0], "bank4")
         for (d, cols, tag), bank in zip(steps, turned):
             weigh_turned(d, cols, bank)
-        back_a = turn_back([prob_turned] + weighed, halves[0], "bank6")
-        back_b = turn_back(weighed, quarters[2], "bank3")
-        back_c = turn_back(weighed, quarters[3], "bank4")
-        copy_back(halves[0], back_a)
+        back_a = turn_back(halves[0], "bank6")
+        back_b = turn_back(quarters[2], "bank3")
+        back_c = turn_back(quarters[3], "bank4")
 
         fetch(0, halves[0])
         fetch(1, halves[0])
@@ -246,6 +233,7 @@ def tile_picked_ycns_one_p_kernel(tc, x_words, x_scales, w1, gate, goal, known, 
         fetch(1, quarters[2])
         fetch(1, quarters[3])
         add_second(quarters[2])
+        add_back(halves[0], back_a)
         add_second(quarters[3])
         add_back(quarters[2], back_b)
         add_back(quarters[3], back_c)

@@ -43,7 +43,7 @@ def tile_picked_ycns_one_p_kernel(tc, x_words, x_scales, w1, gate, goal, known, 
         scale_table = sb.tile([P, T], U8, name="scale_table", align_bytes=64)
         word_table = [sb.tile([P, T], U32, name=f"word_table{o}", align_bytes=64) for o in range(PASSES)]
         goal_t = [sb.tile([P, S], F32, name=f"goal_t{b}") for b in range(2)]
-        gate_t = sb.tile([P, 2, S], F32, name="gate_t")
+        gate_t = [sb.tile([P, S], F32, name=f"gate_t{d}") for d in range(2)]
         known_t = sb.tile([P, PACK], F32, name="known_t")
         gate_runs = sb.tile([P, P], F32, name="gate_runs")
 
@@ -80,7 +80,8 @@ def tile_picked_ycns_one_p_kernel(tc, x_words, x_scales, w1, gate, goal, known, 
         nc.sync.dma_start(pos_t[1][:], pos2)
         nc.sync.dma_start(gate_runs[: 2 * len(quarters), :], gate[:, 0, :].rearrange("d (s n) -> d s n", n=P))
         nc.sync.dma_start(goal_t[1][:], goal[blocks[1], :])
-        nc.sync.dma_start(gate_t[:], gate.rearrange("d p n -> p d n"))
+        nc.sync.dma_start(gate_t[0][:], gate[0])
+        nc.sync.dma_start(gate_t[1][:], gate[1])
 
         known_rows = ps.tile([P, S], F32, name="known_rows", tag="known_bank")
         for t in range(PACK):
@@ -162,7 +163,7 @@ def tile_picked_ycns_one_p_kernel(tc, x_words, x_scales, w1, gate, goal, known, 
         def store(b, cols):
             nc.sync.dma_start(out[blocks[b], cols], results[b][:, cols])
 
-        gate_bank = ps.tile([P, P], F32, name="gate_bank", tag="bank5")
+        gate_bank = ps.tile([P, P], F32, name="gate_bank", tag="bank6")
         nc.tensor.transpose(gate_bank[:], gate_runs[:], ident[:])
         gate_columns = sb.tile([P, 2 * len(quarters)], F32, name="gate_columns")
         nc.scalar.copy(gate_columns[:], gate_bank[:, : 2 * len(quarters)])
@@ -207,7 +208,7 @@ def tile_picked_ycns_one_p_kernel(tc, x_words, x_scales, w1, gate, goal, known, 
         part = sb.tile([P, S], F32, name="part")
 
         def fetch(d, cols):
-            nc.vector.tensor_tensor(term[d][:, cols], errors[1][:].indirect(pos_t[d][:, entries(cols)]), gate_t[:, d, cols], ALU.mult)
+            nc.vector.tensor_tensor(term[d][:, cols], errors[1][:].indirect(pos_t[d][:, entries(cols)]), gate_t[d][:, cols], ALU.mult)
 
         def add_first(cols):
             nc.vector.tensor_tensor(part[:, cols], term[0][:, cols], prob[1][:, cols], ALU.add)
@@ -225,12 +226,12 @@ def tile_picked_ycns_one_p_kernel(tc, x_words, x_scales, w1, gate, goal, known, 
         back_c = turn_back(quarters[3], "bank4")
 
         fetch(0, halves[0])
-        fetch(1, halves[0])
-        add_first(halves[0])
         fetch(0, halves[1])
-        add_second(halves[0])
+        add_first(halves[0])
+        fetch(1, halves[0])
         add_first(halves[1])
         fetch(1, quarters[2])
+        add_second(halves[0])
         fetch(1, quarters[3])
         add_second(quarters[2])
         add_back(halves[0], back_a)

@@ -133,9 +133,20 @@ def tile_picked_ycns_one_p_kernel(tc, x_words, x_scales, w1, gate, goal, known, 
                 stop=(o == PASSES - 1),
             )
 
-        for o in range(PASSES):
-            for i in range(3):
-                multiply(i, o)
+        for i in range(3):
+            multiply(i, 0)
+        unread = ps.tile([P, S], F32, name="unread", tag="bank5")
+        nc.tensor.matmul_mx(
+            out=unread[:],
+            lhsT=w_words[0][:, :P].bitcast(FP8X4),
+            lhsT_scale=w_scales[0][:, :P],
+            rhs=x_words_picked[0][:].bitcast(FP8X4),
+            rhs_scale=x_scales_picked[:],
+            start=True,
+            stop=True,
+        )
+        for i in range(3):
+            multiply(i, 1)
         for i in range(3, 5):
             for o in range(PASSES):
                 multiply(i, o)

@@ -49,10 +49,10 @@ def tile_picked_ycns_one_p_kernel(tc, x_words, x_scales, w1, gate, goal, known, 
 
         nc.vector.memset(scale_table[:].bitcast(I32), 0)
 
-        errors = [sb.tile([P, S + SPARE], F32, name="errors0"), sb.tile([P, S], F32, name="errors1")]
+        errors = [sb.tile([P, S], F32, name="errors0"), sb.tile([P, S + SPARE], F32, name="errors1")]
         zeros = sb.tile([P, SPARE], F32, name="zeros")
         nc.vector.memset(zeros[:], 0.0)
-        nc.scalar.activation(errors[0][:, S:], zeros[:], ACT.Sigmoid)
+        nc.scalar.activation(errors[1][:, S:], zeros[:], ACT.Sigmoid)
         nc.gpsimd.memset(gate_runs[:], 0.0)
         ident = sb.tile([P, P], F32, name="ident")
         make_identity(nc, ident[:])
@@ -163,11 +163,13 @@ def tile_picked_ycns_one_p_kernel(tc, x_words, x_scales, w1, gate, goal, known, 
         def mask(b, cols):
             nc.vector.scalar_tensor_tensor(errors[b][:, cols], diff[b][:, cols], SMOOTH, known_rows[:, cols], ALU.mult, ALU.mult)
 
-        subtract(*pieces[0])
-        for piece, following in zip(pieces, pieces[1:]):
-            subtract(*following)
-            mask(*piece)
-        mask(*pieces[-1])
+        for b in range(2):
+            own = [piece for piece in pieces if piece[0] == b]
+            subtract(*own[0])
+            for piece, following in zip(own, own[1:]):
+                subtract(*following)
+                mask(*piece)
+            mask(*own[-1])
 
         results = [sb.tile([P, S], F32, name=f"result{b}") for b in range(2)]
 
@@ -236,11 +238,9 @@ def tile_picked_ycns_one_p_kernel(tc, x_words, x_scales, w1, gate, goal, known, 
         back_b = turn_back(quarters[2], "bank3")
         back_c = turn_back(quarters[3], "bank4")
 
-        fetch(0, halves[0])
-        fetch(0, halves[1])
-        add_first(halves[0])
+        fetch(0, slice(0, S))
         fetch(1, halves[0])
-        add_first(halves[1])
+        add_first(slice(0, S))
         fetch(1, quarters[2])
         add_second(halves[0])
         fetch(1, quarters[3])

@@ -241,11 +241,9 @@ def tile_picked_ycns_one_p_kernel(tc, x_words, x_scales, w1, gate, goal, known, 
         fetch(0, slice(0, S))
         fetch(1, halves[0])
         add_first(slice(0, S))
-        fetch(1, quarters[2])
+        fetch(1, halves[1])
         add_second(halves[0])
-        fetch(1, quarters[3])
-        add_second(quarters[2])
+        add_second(halves[1])
         add_back(halves[0], back_a)
-        add_second(quarters[3])
         add_back(quarters[2], back_b)
         add_back(quarters[3], back_c)

@@ -105,19 +105,21 @@ def tile_picked_ycns_one_p_kernel(tc, x_words, x_scales, w1, gate, goal, known, 
 
         gather_words(0, slice(0, S))
         nc.vector.tensor_copy(x_scales_picked[:], scale_table[:].indirect(offs_t[:]))
-        grouped00 = sb.tile([P, P * PACK], BF16, name="grouped00", tag="grouped", align_bytes=64)
-        grouped01 = sb.tile([P, P * PACK], BF16, name="grouped01", align_bytes=64)
+        grouped00 = sb.tile([P, P * PACK], BF16, name="grouped00", align_bytes=64)
+        grouped01 = sb.tile([P, P * PACK], BF16, name="grouped01", tag="grouped", align_bytes=64)
         interleave(grouped00[:], w_pass0[:, :, blocks[0]])
         interleave(grouped01[:], w_pass1_block0[:])
         quantize(0, slice(0, P), grouped00[:])
         quantize(0, slice(P, 2 * P), grouped01[:])
-        grouped1 = sb.tile([P, PASSES * P * PACK], BF16, name="grouped1", tag="grouped", align_bytes=64)
-        interleave(grouped1[:, : P * PACK], w_pass0[:, :, blocks[1]])
-        interleave(grouped1[:, P * PACK :], w_pass1_block1[:])
-        for b, cols in pieces:
-            if b == 0:
-                gather_words(1, cols)
-        quantize(1, slice(0, 2 * P), grouped1[:])
+        grouped10 = sb.tile([P, P * PACK], BF16, name="grouped10", tag="grouped", align_bytes=64)
+        grouped11 = sb.tile([P, P * PACK], BF16, name="grouped11", align_bytes=64)
+        interleave(grouped10[:], w_pass0[:, :, blocks[1]])
+        interleave(grouped11[:], w_pass1_block1[:])
+        gather_words(1, pieces[0][1])
+        quantize(1, slice(0, P), grouped10[:])
+        gather_words(1, pieces[1][1])
+        gather_words(1, pieces[2][1])
+        quantize(1, slice(P, 2 * P), grouped11[:])
 
         logits = [ps.tile([P, cols.stop - cols.start], F32, name=f"logits{i}", tag=f"bank{i}") for i, (b, cols) in enumerate(pieces)]
 
@@ -135,21 +137,11 @@ def tile_picked_ycns_one_p_kernel(tc, x_words, x_scales, w1, gate, goal, known, 
 
         for i in range(3):
             multiply(i, 0)
-        unread = ps.tile([P, S], F32, name="unread", tag="bank5")
-        nc.tensor.matmul_mx(
-            out=unread[:],
-            lhsT=w_words[0][:, :P].bitcast(FP8X4),
-            lhsT_scale=w_scales[0][:, :P],
-            rhs=x_words_picked[0][:].bitcast(FP8X4),
-            rhs_scale=x_scales_picked[:],
-            start=True,
-            stop=True,
-        )
-        for i in range(3):
+        multiply(0, 1)
+        multiply(3, 0)
+        multiply(4, 0)
+        for i in range(1, len(pieces)):
             multiply(i, 1)
-        for i in range(3, 5):
-            for o in range(PASSES):
-                multiply(i, o)
 
         prob = [sb.tile([P, S], F32, name="prob0", tag=f"w_raw1_{P}"), sb.tile([P, S], F32, name="prob1")]
         for i, (b, cols) in enumerate(pieces):

@@ -75,10 +75,10 @@ def tile_picked_ycns_one_p_kernel(tc, x_words, x_scales, w1, gate, goal, known, 
         w_pass1_block0 = load_w(1, blocks[0])
         load_words(1)
         w_pass1_block1 = load_w(1, blocks[1])
-        nc.sync.dma_start(goal_t[0][:], goal[blocks[0], :])
         nc.sync.dma_start(pos_t[0][:], pos1)
         nc.sync.dma_start(pos_t[1][:], pos2)
         nc.sync.dma_start(gate_runs[: 2 * len(quarters), :], gate[:, 0, :].rearrange("d (s n) -> d s n", n=P))
+        nc.sync.dma_start(goal_t[0][:], goal[blocks[0], :])
         nc.sync.dma_start(goal_t[1][:], goal[blocks[1], :])
         nc.sync.dma_start(gate_t[0][:], gate[0])
         nc.sync.dma_start(gate_t[1][:], gate[1])
@@ -88,7 +88,7 @@ def tile_picked_ycns_one_p_kernel(tc, x_words, x_scales, w1, gate, goal, known, 
             nc.tensor.transpose(known_rows[:, t:S:PACK], known_t[:, t : t + 1].to_broadcast([P, P]), ident[:])
 
         x_scales_picked = sb.tile([P, S], U8, name="x_scales_picked", align_bytes=64)
-        x_words_picked = [sb.tile([P, S], U32, name=f"x_words_picked{o}", align_bytes=64) for o in range(PASSES)]
+        x_words_picked = [sb.tile([P, S], U32, name="x_words_picked0", align_bytes=64)]
         w_words = [sb.tile([P, PASSES * P], U32, name=f"w_words{b}", align_bytes=64) for b in range(2)]
         w_scales = [sb.tile([P, PASSES * P], U8, name=f"w_scales{b}", align_bytes=64) for b in range(2)]
 
@@ -101,7 +101,7 @@ def tile_picked_ycns_one_p_kernel(tc, x_words, x_scales, w1, gate, goal, known, 
         def gather_words(o, cols):
             nc.vector.tensor_copy(x_words_picked[o][:, cols], word_table[o][:].indirect(offs_t[:, entries(cols)]))
 
-        pieces = [(0, quarters[0]), (0, slice(P, 3 * P)), (0, quarters[3]), (1, halves[0]), (1, halves[1])]
+        pieces = [(0, halves[0]), (0, quarters[2]), (0, quarters[3]), (1, halves[0]), (1, halves[1])]
 
         gather_words(0, slice(0, S))
         nc.vector.tensor_copy(x_scales_picked[:], scale_table[:].indirect(offs_t[:]))
@@ -111,14 +111,16 @@ def tile_picked_ycns_one_p_kernel(tc, x_words, x_scales, w1, gate, goal, known, 
         interleave(grouped01[:], w_pass1_block0[:])
         quantize(0, slice(0, P), grouped00[:])
         quantize(0, slice(P, 2 * P), grouped01[:])
-        grouped10 = sb.tile([P, P * PACK], BF16, name="grouped10", tag="grouped", align_bytes=64)
+        grouped10 = sb.tile([P, P * PACK], BF16, name="grouped10", tag="aside", align_bytes=64)
         grouped11 = sb.tile([P, P * PACK], BF16, name="grouped11", align_bytes=64)
-        interleave(grouped10[:], w_pass0[:, :, blocks[1]])
+        nc.gpsimd.tensor_scalar(
+            grouped10[:].rearrange("p (c t) -> p c t", t=PACK), w_pass0[:, :, blocks[1]].rearrange("p t c -> p c t"), 1.0, 0.0, ALU.mult, ALU.add
+        )
         interleave(grouped11[:], w_pass1_block1[:])
-        gather_words(1, pieces[0][1])
         quantize(1, slice(0, P), grouped10[:])
-        gather_words(1, pieces[1][1])
-        gather_words(1, pieces[2][1])
+        x_words_picked.append(sb.tile([P, S], U32, name="x_words_picked1", tag="aside", align_bytes=64))
+        for i in range(3):
+            gather_words(1, pieces[i][1])
         quantize(1, slice(P, 2 * P), grouped11[:])
 
         logits = [ps.tile([P, cols.stop - cols.start], F32, name=f"logits{i}", tag=f"bank{i}") for i, (b, cols) in enumerate(pieces)]
@@ -135,13 +137,9 @@ def tile_picked_ycns_one_p_kernel(tc, x_words, x_scales, w1, gate, goal, known, 
                 stop=(o == PASSES - 1),
             )
 
-        for i in range(3):
-            multiply(i, 0)
-        multiply(0, 1)
-        multiply(3, 0)
-        multiply(4, 0)
-        for i in range(1, len(pieces)):
-            multiply(i, 1)
+        for o in range(PASSES):
+            for i in range(len(pieces)):
+                multiply(i, o)
 
         prob = [sb.tile([P, S], F32, name="prob0", tag=f"w_raw1_{P}"), sb.tile([P, S], F32, name="prob1")]
         for i, (b, cols) in enumerate(pieces):
@@ -156,14 +154,12 @@ def tile_picked_ycns_one_p_kernel(tc, x_words, x_scales, w1, gate, goal, known, 
             nc.vector.scalar_tensor_tensor(errors[b][:, cols], diff[b][:, cols], SMOOTH, known_rows[:, cols], ALU.mult, ALU.mult)
 
         for b in range(2):
-            own = [piece for piece in pieces if piece[0] == b]
-            subtract(*own[0])
-            for piece, following in zip(own, own[1:]):
-                subtract(*following)
-                mask(*piece)
-            mask(*own[-1])
+            for cols in halves:
+                subtract(b, cols)
+            for cols in halves:
+                mask(b, cols)
 
-        results = [sb.tile([P, S], F32, name=f"result{b}") for b in range(2)]
+        results = [None, sb.tile([P, S], F32, name="result1")]
 
         def store(b, cols):
             nc.sync.dma_start(out[blocks[b], cols], results[b][:, cols])
@@ -173,21 +169,21 @@ def tile_picked_ycns_one_p_kernel(tc, x_words, x_scales, w1, gate, goal, known, 
         gate_columns = sb.tile([P, 2 * len(quarters)], F32, name="gate_columns")
         nc.scalar.copy(gate_columns[:], gate_bank[:, : 2 * len(quarters)])
 
-        fetched = [sb.tile([P, S], F32, name=f"fetched{d}") for d in range(2)]
-        weighed = [sb.tile([P, S], F32, name=f"weighed{d}") for d in range(2)]
+        weighed = [[sb.tile([P, P], F32, name=f"weighed{d}{q}", tag=f"weighed{d}{q}") for q in range(4)] for d in range(2)]
 
-        def fetch_and_turn(d, cols, tag):
-            nc.scalar.activation(fetched[d][:, cols], errors[0][:].indirect(pos_t[d][:, entries(cols)]), ACT.Copy)
+        def fetch_and_turn(d, cols, tag, buffer):
+            fetched = sb.tile([P, cols.stop - cols.start], F32, name=f"fetched{d}_{cols.start}", tag=buffer)
+            nc.scalar.activation(fetched[:], errors[0][:].indirect(pos_t[d][:, entries(cols)]), ACT.Copy)
             bank = ps.tile([P, cols.stop - cols.start], F32, name=f"turned{d}_{cols.start}", tag=tag)
             for c in range(cols.start, cols.stop, P):
-                nc.tensor.transpose(bank[:, c - cols.start : c - cols.start + P], fetched[d][:, c : c + P], ident[:])
+                nc.tensor.transpose(bank[:, c - cols.start : c - cols.start + P], fetched[:, c - cols.start : c - cols.start + P], ident[:])
             return bank
 
         def weigh_turned(d, cols, bank):
             for c in range(cols.start, cols.stop, P):
                 column = len(quarters) * d + c // P
                 nc.scalar.activation(
-                    weighed[d][:, c : c + P], bank[:, c - cols.start : c - cols.start + P], ACT.Copy, scale=gate_columns[:, column : column + 1]
+                    weighed[d][c // P][:], bank[:, c - cols.start : c - cols.start + P], ACT.Copy, scale=gate_columns[:, column : column + 1]
                 )
 
         def turn_back(cols, tag):
@@ -197,7 +193,7 @@ def tile_picked_ycns_one_p_kernel(tc, x_words, x_scales, w1, gate, goal, known, 
                 for c in range(0, width, P):
                     nc.tensor.matmul(
                         bank[:, c : c + P],
-                        weighed[d][:, cols.start + c : cols.start + c + P],
+                        weighed[d][(cols.start + c) // P][:],
                         ident[:],
                         is_transpose=True,
                         start=(d == 0 and c == 0),
@@ -209,7 +205,7 @@ def tile_picked_ycns_one_p_kernel(tc, x_words, x_scales, w1, gate, goal, known, 
             nc.vector.tensor_tensor(results[0][:, cols], prob[0][:, cols], bank[:], ALU.add)
             store(0, cols)
 
-        term = [sb.tile([P, S], F32, name=f"term{d}") for d in range(2)]
+        term = [sb.tile([P, S], F32, name=f"term{d}", tag=f"term{d}") for d in range(2)]
         part = sb.tile([P, S], F32, name="part")
 
         def fetch(d, cols):
@@ -222,20 +218,25 @@ def tile_picked_ycns_one_p_kernel(tc, x_words, x_scales, w1, gate, goal, known, 
             nc.vector.tensor_tensor(results[1][:, cols], part[:, cols], term[1][:, cols], ALU.add)
             store(1, cols)
 
-        steps = [(0, halves[0], "bank0"), (1, halves[0], "bank1"), (0, halves[1], "bank2"), (1, halves[1], "bank5")]
-        turned = [fetch_and_turn(*step) for step in steps]
-        for (d, cols, tag), bank in zip(steps, turned):
-            weigh_turned(d, cols, bank)
+        turned00 = fetch_and_turn(0, halves[0], "bank0", "fetched00")
+        turned10 = fetch_and_turn(1, halves[0], "bank1", "fetched10")
+        turned01 = fetch_and_turn(0, halves[1], "bank2", "fetched01")
+        weigh_turned(0, halves[0], turned00)
+        weigh_turned(1, halves[0], turned10)
         back_a = turn_back(halves[0], "bank6")
+        turned11 = fetch_and_turn(1, halves[1], "bank5", "fetched11")
+        weigh_turned(0, halves[1], turned01)
+        weigh_turned(1, halves[1], turned11)
         back_b = turn_back(quarters[2], "bank3")
         back_c = turn_back(quarters[3], "bank4")
 
         fetch(0, slice(0, S))
         fetch(1, halves[0])
         add_first(slice(0, S))
+        results[0] = sb.tile([P, S], F32, name="result0", tag="term0")
         fetch(1, halves[1])
         add_second(halves[0])
-        add_second(halves[1])
         add_back(halves[0], back_a)
+        add_second(halves[1])
         add_back(quarters[2], back_b)
         add_back(quarters[3], back_c)

@@ -141,7 +141,7 @@ def tile_picked_ycns_one_p_kernel(tc, x_words, x_scales, w1, gate, goal, known, 
             for i in range(len(pieces)):
                 multiply(i, o)
 
-        prob = [sb.tile([P, S], F32, name="prob0", tag=f"w_raw1_{P}"), sb.tile([P, S], F32, name="prob1")]
+        prob = [sb.tile([P, S], F32, name="prob0"), sb.tile([P, S], F32, name="prob1")]
         for i, (b, cols) in enumerate(pieces):
             nc.scalar.activation(prob[b][:, cols], logits[i][:], ACT.Sigmoid)
 

@@ -42,7 +42,7 @@ def tile_picked_ycns_one_p_kernel(tc, x_words, x_scales, w1, gate, goal, known, 
         pos_t = [sb.tile([P, S // PER_COLUMN], U16, name=f"pos_t{d}") for d in range(2)]
         scale_table = sb.tile([P, T], U8, name="scale_table", align_bytes=64)
         word_table = [sb.tile([P, T], U32, name=f"word_table{o}", align_bytes=64) for o in range(PASSES)]
-        goal_t = [sb.tile([P, S], F32, name=f"goal_t{b}") for b in range(2)]
+        goal_t = [sb.tile([P, S], F32, name=f"goal_t{b}", tag=f"goal{b}") for b in range(2)]
         gate_t = [sb.tile([P, S], F32, name=f"gate_t{d}") for d in range(2)]
         known_t = sb.tile([P, PACK], F32, name="known_t")
         gate_runs = sb.tile([P, P], F32, name="gate_runs")
@@ -145,7 +145,7 @@ def tile_picked_ycns_one_p_kernel(tc, x_words, x_scales, w1, gate, goal, known, 
         for i, (b, cols) in enumerate(pieces):
             nc.scalar.activation(prob[b][:, cols], logits[i][:], ACT.Sigmoid)
 
-        diff = [sb.tile([P, S], F32, name=f"diff{b}") for b in range(2)]
+        diff = [sb.tile([P, S], F32, name=f"diff{b}", tag=f"diff{b}x") for b in range(2)]
 
         def subtract(b, cols):
             nc.vector.tensor_tensor(diff[b][:, cols], goal_t[b][:, cols], prob[b][:, cols], ALU.subtract)
@@ -153,21 +153,34 @@ def tile_picked_ycns_one_p_kernel(tc, x_words, x_scales, w1, gate, goal, known, 
         def mask(b, cols):
             nc.vector.scalar_tensor_tensor(errors[b][:, cols], diff[b][:, cols], SMOOTH, known_rows[:, cols], ALU.mult, ALU.mult)
 
-        for b in range(2):
-            for cols in halves:
-                subtract(b, cols)
-            for cols in halves:
-                mask(b, cols)
+        for cols in halves:
+            subtract(0, cols)
+        for cols in halves:
+            mask(0, cols)
+        nc.gpsimd.tensor_tensor(diff[1][:, halves[0]], goal_t[1][:, halves[0]], prob[1][:, halves[0]], ALU.subtract)
+        subtract(1, halves[1])
+        for cols in halves:
+            mask(1, cols)
+        corner = sb.tile([P, P], F32, name="corner", tag="goal1")
+        nc.vector.tensor_tensor(corner[:], errors[0][:].indirect(pos_t[1][:, entries(quarters[3])]), gate_t[1][:, quarters[3]], ALU.mult)
 
         results = [None, sb.tile([P, S], F32, name="result1")]
 
         def store(b, cols):
             nc.sync.dma_start(out[blocks[b], cols], results[b][:, cols])
 
-        gate_bank = ps.tile([P, P], F32, name="gate_bank", tag="bank6")
-        nc.tensor.transpose(gate_bank[:], gate_runs[:], ident[:])
-        gate_columns = sb.tile([P, 2 * len(quarters)], F32, name="gate_columns")
-        nc.scalar.copy(gate_columns[:], gate_bank[:, : 2 * len(quarters)])
+        side_bank = ps.tile([P, S], F32, name="side_bank", tag="bank6")
+        nc.tensor.transpose(side_bank[:, quarters[3]], gate_runs[:], ident[:])
+        for place, q in enumerate((0, 1, 3)):
+            nc.tensor.transpose(side_bank[:, quarters[place]], prob[0][:, quarters[q]], ident[:])
+        side = sb.tile([P, 3 * P + 8], F32, name="side")
+        nc.scalar.copy(side[:], side_bank[:, : 3 * P + 8])
+        gate_columns = side[:, 3 * P :]
+        back_a = ps.tile([P, S // 2], F32, name="back_a", tag="bank6")
+        back_c = ps.tile([P, P], F32, name="back_c", tag="bank4")
+        for q in range(2):
+            nc.tensor.matmul(back_a[:, quarters[q]], side[:, quarters[q]], ident[:], is_transpose=True, start=(q == 0), stop=False)
+        nc.tensor.matmul(back_c[:], side[:, quarters[2]], ident[:], is_transpose=True, start=True, stop=False)
 
         weighed = [[sb.tile([P, P], F32, name=f"weighed{d}{q}", tag=f"weighed{d}{q}") for q in range(4)] for d in range(2)]
 
@@ -201,10 +214,6 @@ def tile_picked_ycns_one_p_kernel(tc, x_words, x_scales, w1, gate, goal, known, 
                     )
             return bank
 
-        def add_back(cols, bank):
-            nc.vector.tensor_tensor(results[0][:, cols], prob[0][:, cols], bank[:], ALU.add)
-            store(0, cols)
-
         term = [sb.tile([P, S], F32, name=f"term{d}", tag=f"term{d}") for d in range(2)]
         part = sb.tile([P, S], F32, name="part")
 
@@ -223,20 +232,26 @@ def tile_picked_ycns_one_p_kernel(tc, x_words, x_scales, w1, gate, goal, known, 
         turned01 = fetch_and_turn(0, halves[1], "bank2", "fetched01")
         weigh_turned(0, halves[0], turned00)
         weigh_turned(1, halves[0], turned10)
-        back_a = turn_back(halves[0], "bank6")
-        turned11 = fetch_and_turn(1, halves[1], "bank5", "fetched11")
+        for d in range(2):
+            for q in range(2):
+                nc.tensor.matmul(back_a[:, quarters[q]], weighed[d][q][:], ident[:], is_transpose=True, start=False, stop=(d == 1 and q == 1))
+        turned11 = fetch_and_turn(1, quarters[2], "bank5", "fetched11")
         weigh_turned(0, halves[1], turned01)
-        weigh_turned(1, halves[1], turned11)
+        weigh_turned(1, quarters[2], turned11)
+        nc.tensor.matmul(back_c[:], weighed[0][3][:], ident[:], is_transpose=True, start=False, stop=True)
         back_b = turn_back(quarters[2], "bank3")
-        back_c = turn_back(quarters[3], "bank4")
+        joined = sb.tile([P, S // 2], F32, name="joined", tag="fetched11")
+        nc.scalar.copy(joined[:], back_a[:])
+        nc.scalar.dma_start(out[blocks[0], halves[0]], joined[:])
 
         fetch(0, slice(0, S))
         fetch(1, halves[0])
-        add_first(slice(0, S))
+        add_first(halves[0])
+        add_first(halves[1])
         results[0] = sb.tile([P, S], F32, name="result0", tag="term0")
-        fetch(1, halves[1])
         add_second(halves[0])
-        add_back(halves[0], back_a)
+        fetch(1, halves[1])
+        nc.vector.tensor_tensor(results[0][:, quarters[3]], corner[:], back_c[:], ALU.add)
         add_second(halves[1])
-        add_back(quarters[2], back_b)
-        add_back(quarters[3], back_c)
+        nc.vector.tensor_tensor(results[0][:, quarters[2]], prob[0][:, quarters[2]], back_b[:], ALU.add)
+        store(0, halves[1])

@@ -116,7 +116,10 @@ def tile_picked_ycns_one_p_kernel(tc, x_words, x_scales, w1, gate, goal, known, 
         nc.gpsimd.tensor_scalar(
             grouped10[:].rearrange("p (c t) -> p c t", t=PACK), w_pass0[:, :, blocks[1]].rearrange("p t c -> p c t"), 1.0, 0.0, ALU.mult, ALU.add
         )
-        interleave(grouped11[:], w_pass1_block1[:])
+        interleave(grouped11[:, : 2 * P], w_pass1_block1[:, :, : P // 2])
+        nc.gpsimd.tensor_scalar(
+            grouped11[:, 2 * P :].rearrange("p (c t) -> p c t", t=PACK), w_pass1_block1[:, :, P // 2 :].rearrange("p t c -> p c t"), 1.0, 0.0, ALU.mult, ALU.add
+        )
         quantize(1, slice(0, P), grouped10[:])
         x_words_picked.append(sb.tile([P, S], U32, name="x_words_picked1", tag="aside", align_bytes=64))
         for i in range(3):

@@ -37,6 +37,7 @@ def tile_picked_ycns_one_p_kernel(tc, x_words, x_scales, w1, gate, goal, known, 
     with ExitStack() as ctx:
         sb = ctx.enter_context(tc.tile_pool(name="sb", bufs=1))
         ps = ctx.enter_context(tc.psum_pool(name="ps", bufs=1))
+        reused = ctx.enter_context(tc.tile_pool(name="reused", bufs=1))
 
         offs_t = sb.tile([P, S // PER_COLUMN], U16, name="offs_t")
         pos_t = [sb.tile([P, S // PER_COLUMN], U16, name=f"pos_t{d}") for d in range(2)]
@@ -60,8 +61,7 @@ def tile_picked_ycns_one_p_kernel(tc, x_words, x_scales, w1, gate, goal, known, 
         def load_words(o):
             nc.sync.dma_start(word_table[o][:].bitcast(I32), x_words[o].rearrange("p n t -> p (n t)").bitcast(I32))
 
-        def load_w(o, labels):
-            raw = sb.tile([P, PACK, labels.stop - labels.start], F32, name=f"w_raw{o}_{labels.start}")
+        def load_w(o, labels, raw):
             nc.sync.dma_start(raw[:], w1[o * P * PACK : (o + 1) * P * PACK, labels].rearrange("(p t) c -> p t c", t=PACK))
             return raw
 
@@ -71,10 +71,10 @@ def tile_picked_ycns_one_p_kernel(tc, x_words, x_scales, w1, gate, goal, known, 
             live = slice(QUADRANT * q, QUADRANT * q + PASSES * PACK)
             nc.sync.dma_start(scale_table[live, :].bitcast(I32), x_scales[:, PACK * q : PACK * (q + 1), :].bitcast(I32))
         nc.sync.dma_start(known_t[:], known[0].rearrange("(n t) -> n t", t=PACK))
-        w_pass0 = load_w(0, slice(0, N))
-        w_pass1_block0 = load_w(1, blocks[0])
+        w_pass0 = load_w(0, slice(0, N), reused.tile([P, PACK, N], F32, name="w_pass0", offset=0, align_bytes=64))
+        w_pass1_block0 = load_w(1, blocks[0], sb.tile([P, PACK, P], F32, name="w_pass1_block0"))
         load_words(1)
-        w_pass1_block1 = load_w(1, blocks[1])
+        w_pass1_block1 = load_w(1, blocks[1], sb.tile([P, PACK, P], F32, name="w_pass1_block1"))
         nc.sync.dma_start(pos_t[0][:], pos1)
         nc.sync.dma_start(pos_t[1][:], pos2)
         nc.sync.dma_start(gate_runs[: 2 * len(quarters), :], gate[:, 0, :].rearrange("d (s n) -> d s n", n=P))
@@ -88,15 +88,25 @@ def tile_picked_ycns_one_p_kernel(tc, x_words, x_scales, w1, gate, goal, known, 
             nc.tensor.transpose(known_rows[:, t:S:PACK], known_t[:, t : t + 1].to_broadcast([P, P]), ident[:])
 
         x_scales_picked = sb.tile([P, S], U8, name="x_scales_picked", align_bytes=64)
-        x_words_picked = [sb.tile([P, S], U32, name="x_words_picked0", align_bytes=64)]
-        w_words = [sb.tile([P, PASSES * P], U32, name=f"w_words{b}", align_bytes=64) for b in range(2)]
-        w_scales = [sb.tile([P, PASSES * P], U8, name=f"w_scales{b}", align_bytes=64) for b in range(2)]
+        x_words_picked = [
+            sb.tile([P, S], U32, name="x_words_picked0", align_bytes=64),
+            reused.tile([P, S], U32, name="x_words_picked1", offset=0, align_bytes=64),
+        ]
+        pass0_words = sb.tile([P, N], U32, name="pass0_words", align_bytes=64)
+        pass0_scales = sb.tile([P, N], U8, name="pass0_scales", align_bytes=64)
+        pass1_words = [
+            reused.tile([P, P], U32, name="pass1_words0", offset=4 * S, align_bytes=64),
+            sb.tile([P, P], U32, name="pass1_words1", align_bytes=64),
+        ]
+        pass1_scales = [sb.tile([P, P], U8, name=f"pass1_scales{b}", align_bytes=64) for b in range(2)]
+        w_words = [[pass0_words[:, blocks[b]], pass1_words[b][:]] for b in range(2)]
+        w_scales = [[pass0_scales[:, blocks[b]], pass1_scales[b][:]] for b in range(2)]
 
         def interleave(dst, raw):
             nc.scalar.copy(dst.rearrange("p (c i t) -> p c t i", i=4, t=PACK), raw.rearrange("p t (c i) -> p c t i", i=4))
 
-        def quantize(b, cols, grouped):
-            nc.vector.quantize_mx(out=w_words[b][:, cols].bitcast(FP8X4), scales=w_scales[b][:, cols], in_=grouped)
+        def quantize(words, scales, grouped):
+            nc.vector.quantize_mx(out=words.bitcast(FP8X4), scales=scales, in_=grouped)
 
         def gather_words(o, cols):
             nc.vector.tensor_copy(x_words_picked[o][:, cols], word_table[o][:].indirect(offs_t[:, entries(cols)]))
@@ -105,26 +115,23 @@ def tile_picked_ycns_one_p_kernel(tc, x_words, x_scales, w1, gate, goal, known, 
 
         gather_words(0, slice(0, S))
         nc.vector.tensor_copy(x_scales_picked[:], scale_table[:].indirect(offs_t[:]))
-        grouped00 = sb.tile([P, P * PACK], BF16, name="grouped00", align_bytes=64)
-        grouped01 = sb.tile([P, P * PACK], BF16, name="grouped01", tag="grouped", align_bytes=64)
-        interleave(grouped00[:], w_pass0[:, :, blocks[0]])
-        interleave(grouped01[:], w_pass1_block0[:])
-        quantize(0, slice(0, P), grouped00[:])
-        quantize(0, slice(P, 2 * P), grouped01[:])
-        grouped10 = sb.tile([P, P * PACK], BF16, name="grouped10", tag="aside", align_bytes=64)
-        grouped11 = sb.tile([P, P * PACK], BF16, name="grouped11", align_bytes=64)
-        nc.gpsimd.tensor_scalar(
-            grouped10[:].rearrange("p (c t) -> p c t", t=PACK), w_pass0[:, :, blocks[1]].rearrange("p t c -> p c t"), 1.0, 0.0, ALU.mult, ALU.add
-        )
-        interleave(grouped11[:, : 2 * P], w_pass1_block1[:, :, : P // 2])
-        nc.gpsimd.tensor_scalar(
-            grouped11[:, 2 * P :].rearrange("p (c t) -> p c t", t=PACK), w_pass1_block1[:, :, P // 2 :].rearrange("p t c -> p c t"), 1.0, 0.0, ALU.mult, ALU.add
-        )
-        quantize(1, slice(0, P), grouped10[:])
-        x_words_picked.append(sb.tile([P, S], U32, name="x_words_picked1", tag="aside", align_bytes=64))
+        grouped_pass0 = sb.tile([P, N * PACK], BF16, name="grouped_pass0", align_bytes=64)
+        grouped_pass1 = [sb.tile([P, P * PACK], BF16, name=f"grouped_pass1{b}", align_bytes=64) for b in range(2)]
+
+        def interleave_aside(dst, raw):
+            nc.gpsimd.tensor_scalar(dst.rearrange("p (c t) -> p c t", t=PACK), raw.rearrange("p t c -> p c t"), 1.0, 0.0, ALU.mult, ALU.add)
+
+        interleave(grouped_pass0[:, : P * PACK], w_pass0[:, :, blocks[0]])
+        interleave_aside(grouped_pass0[:, P * PACK :], w_pass0[:, :, blocks[1]])
+        interleave(grouped_pass1[0][:], w_pass1_block0[:])
+        interleave(grouped_pass1[1][:, : 2 * P], w_pass1_block1[:, :, : P // 2])
+        interleave_aside(grouped_pass1[1][:, 2 * P :], w_pass1_block1[:, :, P // 2 :])
+        for b in range(2):
+            quantize(w_words[b][0], w_scales[b][0], grouped_pass0[:, b * P * PACK : (b + 1) * P * PACK])
+        quantize(w_words[0][1], w_scales[0][1], grouped_pass1[0][:])
         for i in range(3):
             gather_words(1, pieces[i][1])
-        quantize(1, slice(P, 2 * P), grouped11[:])
+        quantize(w_words[1][1], w_scales[1][1], grouped_pass1[1][:])
 
         logits = [ps.tile([P, cols.stop - cols.start], F32, name=f"logits{i}", tag=f"bank{i}") for i, (b, cols) in enumerate(pieces)]
 
@@ -132,8 +139,8 @@ def tile_picked_ycns_one_p_kernel(tc, x_words, x_scales, w1, gate, goal, known, 
             b, cols = pieces[i]
             nc.tensor.matmul_mx(
                 out=logits[i][:],
-                lhsT=w_words[b][:, o * P : (o + 1) * P].bitcast(FP8X4),
-                lhsT_scale=w_scales[b][:, o * P : (o + 1) * P],
+                lhsT=w_words[b][o].bitcast(FP8X4),
+                lhsT_scale=w_scales[b][o],
                 rhs=x_words_picked[o][:, cols].bitcast(FP8X4),
                 rhs_scale=x_scales_picked[PACK * o :, cols],
                 start=(o == 0),
@@ -165,7 +172,7 @@ def tile_picked_ycns_one_p_kernel(tc, x_words, x_scales, w1, gate, goal, known, 
         for cols in halves:
             mask(1, cols)
         corner = sb.tile([P, P], F32, name="corner", tag="goal1")
-        nc.vector.tensor_tensor(corner[:], errors[0][:].indirect(pos_t[1][:, entries(quarters[3])]), gate_t[1][:, quarters[3]], ALU.mult)
+        nc.vector.tensor_tensor(corner[:], errors[0][:].indirect(pos_t[0][:, entries(quarters[3])]), gate_t[0][:, quarters[3]], ALU.mult)
 
         results = [None, sb.tile([P, S], F32, name="result1")]
 
@@ -205,15 +212,15 @@ def tile_picked_ycns_one_p_kernel(tc, x_words, x_scales, w1, gate, goal, known, 
         def turn_back(cols, tag):
             width = cols.stop - cols.start
             bank = ps.tile([P, width], F32, name=f"back{cols.start}", tag=tag)
-            for d in range(2):
+            for d in (1, 0):
                 for c in range(0, width, P):
                     nc.tensor.matmul(
                         bank[:, c : c + P],
                         weighed[d][(cols.start + c) // P][:],
                         ident[:],
                         is_transpose=True,
-                        start=(d == 0 and c == 0),
-                        stop=(d == 1 and c == width - P),
+                        start=(d == 1 and c == 0),
+                        stop=(d == 0 and c == width - P),
                     )
             return bank
 
@@ -232,16 +239,16 @@ def tile_picked_ycns_one_p_kernel(tc, x_words, x_scales, w1, gate, goal, known, 
 
         turned00 = fetch_and_turn(0, halves[0], "bank0", "fetched00")
         turned10 = fetch_and_turn(1, halves[0], "bank1", "fetched10")
-        turned01 = fetch_and_turn(0, halves[1], "bank2", "fetched01")
+        turned01 = fetch_and_turn(1, halves[1], "bank2", "fetched01")
         weigh_turned(0, halves[0], turned00)
         weigh_turned(1, halves[0], turned10)
         for d in range(2):
             for q in range(2):
                 nc.tensor.matmul(back_a[:, quarters[q]], weighed[d][q][:], ident[:], is_transpose=True, start=False, stop=(d == 1 and q == 1))
-        turned11 = fetch_and_turn(1, quarters[2], "bank5", "fetched11")
-        weigh_turned(0, halves[1], turned01)
-        weigh_turned(1, quarters[2], turned11)
-        nc.tensor.matmul(back_c[:], weighed[0][3][:], ident[:], is_transpose=True, start=False, stop=True)
+        turned11 = fetch_and_turn(0, quarters[2], "bank5", "fetched11")
+        weigh_turned(1, halves[1], turned01)
+        weigh_turned(0, quarters[2], turned11)
+        nc.tensor.matmul(back_c[:], weighed[1][3][:], ident[:], is_transpose=True, start=False, stop=True)
         back_b = turn_back(quarters[2], "bank3")
         joined = sb.tile([P, S // 2], F32, name="joined", tag="fetched11")
         nc.scalar.copy(joined[:], back_a[:])

@@ -262,6 +262,7 @@ def tile_picked_ycns_one_p_kernel(tc, x_words, x_scales, w1, gate, goal, known, 
         add_second(halves[0])
         fetch(1, halves[1])
         nc.vector.tensor_tensor(results[0][:, quarters[3]], corner[:], back_c[:], ALU.add)
+        store(0, quarters[3])
         add_second(halves[1])
         nc.vector.tensor_tensor(results[0][:, quarters[2]], prob[0][:, quarters[2]], back_b[:], ALU.add)
-        store(0, halves[1])
+        store(0, quarters[2])

@@ -75,10 +75,10 @@ def tile_picked_ycns_one_p_kernel(tc, x_words, x_scales, w1, gate, goal, known, 
         w_pass1_block0 = load_w(1, blocks[0], sb.tile([P, PACK, P], F32, name="w_pass1_block0"))
         load_words(1)
         w_pass1_block1 = load_w(1, blocks[1], sb.tile([P, PACK, P], F32, name="w_pass1_block1"))
+        nc.sync.dma_start(goal_t[0][:], goal[blocks[0], :])
+        nc.sync.dma_start(gate_runs[: 2 * len(quarters), :], gate[:, 0, :].rearrange("d (s n) -> d s n", n=P))
         nc.sync.dma_start(pos_t[0][:], pos1)
         nc.sync.dma_start(pos_t[1][:], pos2)
-        nc.sync.dma_start(gate_runs[: 2 * len(quarters), :], gate[:, 0, :].rearrange("d (s n) -> d s n", n=P))
-        nc.sync.dma_start(goal_t[0][:], goal[blocks[0], :])
         nc.sync.dma_start(goal_t[1][:], goal[blocks[1], :])
         nc.sync.dma_start(gate_t[0][:], gate[0])
         nc.sync.dma_start(gate_t[1][:], gate[1])

@@ -22,12 +22,14 @@ PACK = 4
 PASSES = K // (P * PACK)
 PER_COLUMN = 16
 SPARE = 8
+GATE_COLUMNS = 2 * S // P
+SCALAR_SHARE = 80
 SMOOTH = 0.7
 
 
 def tile_picked_ycns_one_p_kernel(tc, x_words, x_scales, w1, gate, goal, known, offs, pos1, pos2, out):
     nc = tc.nc
-    blocks = [slice(0, P), slice(P, N)]
+    panels = [slice(0, P), slice(P, N)]
     halves = [slice(0, S // 2), slice(S // 2, S)]
     quarters = [slice(q * P, (q + 1) * P) for q in range(S // P)]
 
@@ -72,14 +74,14 @@ def tile_picked_ycns_one_p_kernel(tc, x_words, x_scales, w1, gate, goal, known, 
             nc.sync.dma_start(scale_table[live, :].bitcast(I32), x_scales[:, PACK * q : PACK * (q + 1), :].bitcast(I32))
         nc.sync.dma_start(known_t[:], known[0].rearrange("(n t) -> n t", t=PACK))
         w_pass0 = load_w(0, slice(0, N), reused.tile([P, PACK, N], F32, name="w_pass0", offset=0, align_bytes=64))
-        w_pass1_block0 = load_w(1, blocks[0], sb.tile([P, PACK, P], F32, name="w_pass1_block0"))
+        w_pass1_panel0 = load_w(1, panels[0], sb.tile([P, PACK, P], F32, name="w_pass1_panel0"))
         load_words(1)
-        w_pass1_block1 = load_w(1, blocks[1], sb.tile([P, PACK, P], F32, name="w_pass1_block1"))
-        nc.sync.dma_start(goal_t[0][:], goal[blocks[0], :])
-        nc.sync.dma_start(gate_runs[: 2 * len(quarters), :], gate[:, 0, :].rearrange("d (s n) -> d s n", n=P))
+        w_pass1_panel1 = load_w(1, panels[1], sb.tile([P, PACK, P], F32, name="w_pass1_panel1"))
+        nc.sync.dma_start(goal_t[0][:], goal[panels[0], :])
+        nc.sync.dma_start(gate_runs[:GATE_COLUMNS, :], gate[:, 0, :].rearrange("d (s n) -> d s n", n=P))
         nc.sync.dma_start(pos_t[0][:], pos1)
         nc.sync.dma_start(pos_t[1][:], pos2)
-        nc.sync.dma_start(goal_t[1][:], goal[blocks[1], :])
+        nc.sync.dma_start(goal_t[1][:], goal[panels[1], :])
         nc.sync.dma_start(gate_t[0][:], gate[0])
         nc.sync.dma_start(gate_t[1][:], gate[1])
 
@@ -99,8 +101,8 @@ def tile_picked_ycns_one_p_kernel(tc, x_words, x_scales, w1, gate, goal, known, 
             sb.tile([P, P], U32, name="pass1_words1", align_bytes=64),
         ]
         pass1_scales = [sb.tile([P, P], U8, name=f"pass1_scales{b}", align_bytes=64) for b in range(2)]
-        w_words = [[pass0_words[:, blocks[b]], pass1_words[b][:]] for b in range(2)]
-        w_scales = [[pass0_scales[:, blocks[b]], pass1_scales[b][:]] for b in range(2)]
+        w_words = [[pass0_words[:, panels[b]], pass1_words[b][:]] for b in range(2)]
+        w_scales = [[pass0_scales[:, panels[b]], pass1_scales[b][:]] for b in range(2)]
 
         def interleave(dst, raw):
             nc.scalar.copy(dst.rearrange("p (c i t) -> p c t i", i=4, t=PACK), raw.rearrange("p t (c i) -> p c t i", i=4))
@@ -121,16 +123,16 @@ def tile_picked_ycns_one_p_kernel(tc, x_words, x_scales, w1, gate, goal, known, 
         def interleave_aside(dst, raw):
             nc.gpsimd.tensor_scalar(dst.rearrange("p (c t) -> p c t", t=PACK), raw.rearrange("p t c -> p c t"), 1.0, 0.0, ALU.mult, ALU.add)
 
-        interleave(grouped_pass0[:, : P * PACK], w_pass0[:, :, blocks[0]])
-        interleave_aside(grouped_pass0[:, P * PACK :], w_pass0[:, :, blocks[1]])
-        interleave(grouped_pass1[0][:], w_pass1_block0[:])
-        interleave(grouped_pass1[1][:, : 2 * P], w_pass1_block1[:, :, : P // 2])
-        interleave_aside(grouped_pass1[1][:, 2 * P :], w_pass1_block1[:, :, P // 2 :])
+        interleave(grouped_pass0[:, : P * PACK], w_pass0[:, :, panels[0]])
+        interleave_aside(grouped_pass0[:, P * PACK :], w_pass0[:, :, panels[1]])
+        interleave(grouped_pass1[0][:], w_pass1_panel0[:])
+        interleave(grouped_pass1[1][:, : SCALAR_SHARE * PACK], w_pass1_panel1[:, :, :SCALAR_SHARE])
+        interleave_aside(grouped_pass1[1][:, SCALAR_SHARE * PACK :], w_pass1_panel1[:, :, SCALAR_SHARE:])
         for b in range(2):
             quantize(w_words[b][0], w_scales[b][0], grouped_pass0[:, b * P * PACK : (b + 1) * P * PACK])
         quantize(w_words[0][1], w_scales[0][1], grouped_pass1[0][:])
-        for i in range(3):
-            gather_words(1, pieces[i][1])
+        for cols in (halves[0], quarters[2], quarters[3]):
+            gather_words(1, cols)
         quantize(w_words[1][1], w_scales[1][1], grouped_pass1[1][:])
 
         logits = [ps.tile([P, cols.stop - cols.start], F32, name=f"logits{i}", tag=f"bank{i}") for i, (b, cols) in enumerate(pieces)]
@@ -174,25 +176,23 @@ def tile_picked_ycns_one_p_kernel(tc, x_words, x_scales, w1, gate, goal, known, 
         corner = sb.tile([P, P], F32, name="corner", tag="goal1")
         nc.vector.tensor_tensor(corner[:], errors[0][:].indirect(pos_t[0][:, entries(quarters[3])]), gate_t[0][:, quarters[3]], ALU.mult)
 
-        results = [None, sb.tile([P, S], F32, name="result1")]
+        result1 = sb.tile([P, S], F32, name="result1")
 
-        def store(b, cols):
-            nc.sync.dma_start(out[blocks[b], cols], results[b][:, cols])
-
+        joined_quarters = (0, 1, 3)
         side_bank = ps.tile([P, S], F32, name="side_bank", tag="bank6")
         nc.tensor.transpose(side_bank[:, quarters[3]], gate_runs[:], ident[:])
-        for place, q in enumerate((0, 1, 3)):
+        for place, q in enumerate(joined_quarters):
             nc.tensor.transpose(side_bank[:, quarters[place]], prob[0][:, quarters[q]], ident[:])
-        side = sb.tile([P, 3 * P + 8], F32, name="side")
-        nc.scalar.copy(side[:], side_bank[:, : 3 * P + 8])
-        gate_columns = side[:, 3 * P :]
-        back_a = ps.tile([P, S // 2], F32, name="back_a", tag="bank6")
-        back_c = ps.tile([P, P], F32, name="back_c", tag="bank4")
+        side = sb.tile([P, len(joined_quarters) * P + GATE_COLUMNS], F32, name="side")
+        nc.scalar.copy(side[:], side_bank[:, : len(joined_quarters) * P + GATE_COLUMNS])
+        gate_columns = side[:, len(joined_quarters) * P :]
+        sum_half0 = ps.tile([P, S // 2], F32, name="sum_half0", tag="bank6")
+        sum_quarter3 = ps.tile([P, P], F32, name="sum_quarter3", tag="bank4")
         for q in range(2):
-            nc.tensor.matmul(back_a[:, quarters[q]], side[:, quarters[q]], ident[:], is_transpose=True, start=(q == 0), stop=False)
-        nc.tensor.matmul(back_c[:], side[:, quarters[2]], ident[:], is_transpose=True, start=True, stop=False)
+            nc.tensor.matmul(sum_half0[:, quarters[q]], side[:, quarters[q]], ident[:], is_transpose=True, start=(q == 0), stop=False)
+        nc.tensor.matmul(sum_quarter3[:], side[:, quarters[2]], ident[:], is_transpose=True, start=True, stop=False)
 
-        weighed = [[sb.tile([P, P], F32, name=f"weighed{d}{q}", tag=f"weighed{d}{q}") for q in range(4)] for d in range(2)]
+        weighed = [[sb.tile([P, P], F32, name=f"weighed{d}{q}", tag=f"weighed{d}{q}") for q in range(len(quarters))] for d in range(2)]
 
         def fetch_and_turn(d, cols, tag, buffer):
             fetched = sb.tile([P, cols.stop - cols.start], F32, name=f"fetched{d}_{cols.start}", tag=buffer)
@@ -209,21 +209,6 @@ def tile_picked_ycns_one_p_kernel(tc, x_words, x_scales, w1, gate, goal, known, 
                     weighed[d][c // P][:], bank[:, c - cols.start : c - cols.start + P], ACT.Copy, scale=gate_columns[:, column : column + 1]
                 )
 
-        def turn_back(cols, tag):
-            width = cols.stop - cols.start
-            bank = ps.tile([P, width], F32, name=f"back{cols.start}", tag=tag)
-            for d in (1, 0):
-                for c in range(0, width, P):
-                    nc.tensor.matmul(
-                        bank[:, c : c + P],
-                        weighed[d][(cols.start + c) // P][:],
-                        ident[:],
-                        is_transpose=True,
-                        start=(d == 1 and c == 0),
-                        stop=(d == 0 and c == width - P),
-                    )
-            return bank
-
         term = [sb.tile([P, S], F32, name=f"term{d}", tag=f"term{d}") for d in range(2)]
         part = sb.tile([P, S], F32, name="part")
 
@@ -234,35 +219,39 @@ def tile_picked_ycns_one_p_kernel(tc, x_words, x_scales, w1, gate, goal, known, 
             nc.vector.tensor_tensor(part[:, cols], term[0][:, cols], prob[1][:, cols], ALU.add)
 
         def add_second(cols):
-            nc.vector.tensor_tensor(results[1][:, cols], part[:, cols], term[1][:, cols], ALU.add)
-            store(1, cols)
+            nc.vector.tensor_tensor(result1[:, cols], part[:, cols], term[1][:, cols], ALU.add)
+            nc.sync.dma_start(out[panels[1], cols], result1[:, cols])
 
-        turned00 = fetch_and_turn(0, halves[0], "bank0", "fetched00")
-        turned10 = fetch_and_turn(1, halves[0], "bank1", "fetched10")
-        turned01 = fetch_and_turn(1, halves[1], "bank2", "fetched01")
-        weigh_turned(0, halves[0], turned00)
-        weigh_turned(1, halves[0], turned10)
+        list0_half0 = fetch_and_turn(0, halves[0], "bank0", "fetched00")
+        list1_half0 = fetch_and_turn(1, halves[0], "bank1", "fetched10")
+        list1_half1 = fetch_and_turn(1, halves[1], "bank2", "fetched01")
+        weigh_turned(0, halves[0], list0_half0)
+        weigh_turned(1, halves[0], list1_half0)
         for d in range(2):
             for q in range(2):
-                nc.tensor.matmul(back_a[:, quarters[q]], weighed[d][q][:], ident[:], is_transpose=True, start=False, stop=(d == 1 and q == 1))
-        turned11 = fetch_and_turn(0, quarters[2], "bank5", "fetched11")
-        weigh_turned(1, halves[1], turned01)
-        weigh_turned(0, quarters[2], turned11)
-        nc.tensor.matmul(back_c[:], weighed[1][3][:], ident[:], is_transpose=True, start=False, stop=True)
-        back_b = turn_back(quarters[2], "bank3")
-        joined = sb.tile([P, S // 2], F32, name="joined", tag="fetched11")
-        nc.scalar.copy(joined[:], back_a[:])
-        nc.scalar.dma_start(out[blocks[0], halves[0]], joined[:])
+                nc.tensor.matmul(sum_half0[:, quarters[q]], weighed[d][q][:], ident[:], is_transpose=True, start=False, stop=(d == 1 and q == 1))
+        list0_quarter2 = fetch_and_turn(0, quarters[2], "bank5", "fetched11")
+        weigh_turned(1, halves[1], list1_half1)
+        weigh_turned(0, quarters[2], list0_quarter2)
+        nc.tensor.matmul(sum_quarter3[:], weighed[1][3][:], ident[:], is_transpose=True, start=False, stop=True)
+        sum_quarter2 = ps.tile([P, P], F32, name="sum_quarter2", tag="bank3")
+        for d in (1, 0):
+            nc.tensor.matmul(sum_quarter2[:], weighed[d][2][:], ident[:], is_transpose=True, start=(d == 1), stop=(d == 0))
+        result0_half0 = sb.tile([P, S // 2], F32, name="result0_half0", tag="fetched11")
+        nc.scalar.copy(result0_half0[:], sum_half0[:])
+        nc.scalar.dma_start(out[panels[0], halves[0]], result0_half0[:])
+
+        def finish_quarter(q, missing, bank):
+            nc.vector.tensor_tensor(result0[:, quarters[q]], missing, bank[:], ALU.add)
+            nc.sync.dma_start(out[panels[0], quarters[q]], result0[:, quarters[q]])
 
         fetch(0, slice(0, S))
         fetch(1, halves[0])
         add_first(halves[0])
         add_first(halves[1])
-        results[0] = sb.tile([P, S], F32, name="result0", tag="term0")
+        result0 = sb.tile([P, S], F32, name="result0", tag="term0")
         add_second(halves[0])
         fetch(1, halves[1])
-        nc.vector.tensor_tensor(results[0][:, quarters[3]], corner[:], back_c[:], ALU.add)
-        store(0, quarters[3])
+        finish_quarter(3, corner[:], sum_quarter3)
         add_second(halves[1])
-        nc.vector.tensor_tensor(results[0][:, quarters[2]], prob[0][:, quarters[2]], back_b[:], ALU.add)
-        store(0, quarters[2])
+        finish_quarter(2, prob[0][:, quarters[2]], sum_quarter2)

from contextlib import ExitStack

import concourse.mybir as mybir
from concourse.masks import make_identity

K, T, S, N = 1024, 1024, 512, 256
FLOPS = 2 * K * S * N

F32 = mybir.dt.float32
BF16 = mybir.dt.bfloat16
I32 = mybir.dt.int32
U32 = mybir.dt.uint32
U16 = mybir.dt.uint16
U8 = mybir.dt.uint8
FP8X4 = mybir.dt.float8_e4m3fn_x4
ACT = mybir.ActivationFunctionType
ALU = mybir.AluOpType

P = 128
QUADRANT = 32
PACK = 4
PASSES = K // (P * PACK)
PER_COLUMN = 16
SPARE = 8
GATE_COLUMNS = 2 * S // P
SCALAR_SHARE = 80
SMOOTH = 0.7


def tile_picked_ycns_one_p_kernel(tc, x_words, x_scales, w1, gate, goal, known, offs, pos1, pos2, out):
    nc = tc.nc
    panels = [slice(0, P), slice(P, N)]
    halves = [slice(0, S // 2), slice(S // 2, S)]
    quarters = [slice(q * P, (q + 1) * P) for q in range(S // P)]

    def entries(cols):
        return slice(cols.start // PER_COLUMN, cols.stop // PER_COLUMN)

    with ExitStack() as ctx:
        sb = ctx.enter_context(tc.tile_pool(name="sb", bufs=1))
        ps = ctx.enter_context(tc.psum_pool(name="ps", bufs=1))
        reused = ctx.enter_context(tc.tile_pool(name="reused", bufs=1))

        offs_t = sb.tile([P, S // PER_COLUMN], U16, name="offs_t")
        pos_t = [sb.tile([P, S // PER_COLUMN], U16, name=f"pos_t{d}") for d in range(2)]
        scale_table = sb.tile([P, T], U8, name="scale_table", align_bytes=64)
        word_table = [sb.tile([P, T], U32, name=f"word_table{o}", align_bytes=64) for o in range(PASSES)]
        goal_t = [sb.tile([P, S], F32, name=f"goal_t{b}", tag=f"goal{b}") for b in range(2)]
        gate_t = [sb.tile([P, S], F32, name=f"gate_t{d}") for d in range(2)]
        known_t = sb.tile([P, PACK], F32, name="known_t")
        gate_runs = sb.tile([P, P], F32, name="gate_runs")

        nc.vector.memset(scale_table[:].bitcast(I32), 0)

        errors = [sb.tile([P, S], F32, name="errors0"), sb.tile([P, S + SPARE], F32, name="errors1")]
        zeros = sb.tile([P, SPARE], F32, name="zeros")
        nc.vector.memset(zeros[:], 0.0)
        nc.scalar.activation(errors[1][:, S:], zeros[:], ACT.Sigmoid)
        nc.gpsimd.memset(gate_runs[:], 0.0)
        ident = sb.tile([P, P], F32, name="ident")
        make_identity(nc, ident[:])

        def load_words(o):
            nc.sync.dma_start(word_table[o][:].bitcast(I32), x_words[o].rearrange("p n t -> p (n t)").bitcast(I32))

        def load_w(o, labels, raw):
            nc.sync.dma_start(raw[:], w1[o * P * PACK : (o + 1) * P * PACK, labels].rearrange("(p t) c -> p t c", t=PACK))
            return raw

        nc.sync.dma_start(offs_t[:], offs)
        load_words(0)
        for q in range(P // QUADRANT):
            live = slice(QUADRANT * q, QUADRANT * q + PASSES * PACK)
            nc.sync.dma_start(scale_table[live, :].bitcast(I32), x_scales[:, PACK * q : PACK * (q + 1), :].bitcast(I32))
        nc.sync.dma_start(known_t[:], known[0].rearrange("(n t) -> n t", t=PACK))
        w_pass0 = load_w(0, slice(0, N), reused.tile([P, PACK, N], F32, name="w_pass0", offset=0, align_bytes=64))
        w_pass1_panel0 = load_w(1, panels[0], sb.tile([P, PACK, P], F32, name="w_pass1_panel0"))
        load_words(1)
        w_pass1_panel1 = load_w(1, panels[1], sb.tile([P, PACK, P], F32, name="w_pass1_panel1"))
        nc.sync.dma_start(goal_t[0][:], goal[panels[0], :])
        nc.sync.dma_start(gate_runs[:GATE_COLUMNS, :], gate[:, 0, :].rearrange("d (s n) -> d s n", n=P))
        nc.sync.dma_start(pos_t[0][:], pos1)
        nc.sync.dma_start(pos_t[1][:], pos2)
        nc.sync.dma_start(goal_t[1][:], goal[panels[1], :])
        nc.sync.dma_start(gate_t[0][:], gate[0])
        nc.sync.dma_start(gate_t[1][:], gate[1])

        known_rows = ps.tile([P, S], F32, name="known_rows", tag="known_bank")
        for t in range(PACK):
            nc.tensor.transpose(known_rows[:, t:S:PACK], known_t[:, t : t + 1].to_broadcast([P, P]), ident[:])

        x_scales_picked = sb.tile([P, S], U8, name="x_scales_picked", align_bytes=64)
        x_words_picked = [
            sb.tile([P, S], U32, name="x_words_picked0", align_bytes=64),
            reused.tile([P, S], U32, name="x_words_picked1", offset=0, align_bytes=64),
        ]
        pass0_words = sb.tile([P, N], U32, name="pass0_words", align_bytes=64)
        pass0_scales = sb.tile([P, N], U8, name="pass0_scales", align_bytes=64)
        pass1_words = [
            reused.tile([P, P], U32, name="pass1_words0", offset=4 * S, align_bytes=64),
            sb.tile([P, P], U32, name="pass1_words1", align_bytes=64),
        ]
        pass1_scales = [sb.tile([P, P], U8, name=f"pass1_scales{b}", align_bytes=64) for b in range(2)]
        w_words = [[pass0_words[:, panels[b]], pass1_words[b][:]] for b in range(2)]
        w_scales = [[pass0_scales[:, panels[b]], pass1_scales[b][:]] for b in range(2)]

        def interleave(dst, raw):
            nc.scalar.copy(dst.rearrange("p (c i t) -> p c t i", i=4, t=PACK), raw.rearrange("p t (c i) -> p c t i", i=4))

        def quantize(words, scales, grouped):
            nc.vector.quantize_mx(out=words.bitcast(FP8X4), scales=scales, in_=grouped)

        def gather_words(o, cols):
            nc.vector.tensor_copy(x_words_picked[o][:, cols], word_table[o][:].indirect(offs_t[:, entries(cols)]))

        pieces = [(0, halves[0]), (0, quarters[2]), (0, quarters[3]), (1, halves[0]), (1, halves[1])]

        gather_words(0, slice(0, S))
        nc.vector.tensor_copy(x_scales_picked[:], scale_table[:].indirect(offs_t[:]))
        grouped_pass0 = sb.tile([P, N * PACK], BF16, name="grouped_pass0", align_bytes=64)
        grouped_pass1 = [sb.tile([P, P * PACK], BF16, name=f"grouped_pass1{b}", align_bytes=64) for b in range(2)]

        def interleave_aside(dst, raw):
            nc.gpsimd.tensor_scalar(dst.rearrange("p (c t) -> p c t", t=PACK), raw.rearrange("p t c -> p c t"), 1.0, 0.0, ALU.mult, ALU.add)

        interleave(grouped_pass0[:, : P * PACK], w_pass0[:, :, panels[0]])
        interleave_aside(grouped_pass0[:, P * PACK :], w_pass0[:, :, panels[1]])
        interleave(grouped_pass1[0][:], w_pass1_panel0[:])
        interleave(grouped_pass1[1][:, : SCALAR_SHARE * PACK], w_pass1_panel1[:, :, :SCALAR_SHARE])
        interleave_aside(grouped_pass1[1][:, SCALAR_SHARE * PACK :], w_pass1_panel1[:, :, SCALAR_SHARE:])
        for b in range(2):
            quantize(w_words[b][0], w_scales[b][0], grouped_pass0[:, b * P * PACK : (b + 1) * P * PACK])
        quantize(w_words[0][1], w_scales[0][1], grouped_pass1[0][:])
        for cols in (halves[0], quarters[2], quarters[3]):
            gather_words(1, cols)
        quantize(w_words[1][1], w_scales[1][1], grouped_pass1[1][:])

        logits = [ps.tile([P, cols.stop - cols.start], F32, name=f"logits{i}", tag=f"bank{i}") for i, (b, cols) in enumerate(pieces)]

        def multiply(i, o):
            b, cols = pieces[i]
            nc.tensor.matmul_mx(
                out=logits[i][:],
                lhsT=w_words[b][o].bitcast(FP8X4),
                lhsT_scale=w_scales[b][o],
                rhs=x_words_picked[o][:, cols].bitcast(FP8X4),
                rhs_scale=x_scales_picked[PACK * o :, cols],
                start=(o == 0),
                stop=(o == PASSES - 1),
            )

        for o in range(PASSES):
            for i in range(len(pieces)):
                multiply(i, o)

        prob = [sb.tile([P, S], F32, name="prob0"), sb.tile([P, S], F32, name="prob1")]
        for i, (b, cols) in enumerate(pieces):
            nc.scalar.activation(prob[b][:, cols], logits[i][:], ACT.Sigmoid)

        diff = [sb.tile([P, S], F32, name=f"diff{b}", tag=f"diff{b}x") for b in range(2)]

        def subtract(b, cols):
            nc.vector.tensor_tensor(diff[b][:, cols], goal_t[b][:, cols], prob[b][:, cols], ALU.subtract)

        def mask(b, cols):
            nc.vector.scalar_tensor_tensor(errors[b][:, cols], diff[b][:, cols], SMOOTH, known_rows[:, cols], ALU.mult, ALU.mult)

        for cols in halves:
            subtract(0, cols)
        for cols in halves:
            mask(0, cols)
        nc.gpsimd.tensor_tensor(diff[1][:, halves[0]], goal_t[1][:, halves[0]], prob[1][:, halves[0]], ALU.subtract)
        subtract(1, halves[1])
        for cols in halves:
            mask(1, cols)
        corner = sb.tile([P, P], F32, name="corner", tag="goal1")
        nc.vector.tensor_tensor(corner[:], errors[0][:].indirect(pos_t[0][:, entries(quarters[3])]), gate_t[0][:, quarters[3]], ALU.mult)

        result1 = sb.tile([P, S], F32, name="result1")

        joined_quarters = (0, 1, 3)
        side_bank = ps.tile([P, S], F32, name="side_bank", tag="bank6")
        nc.tensor.transpose(side_bank[:, quarters[3]], gate_runs[:], ident[:])
        for place, q in enumerate(joined_quarters):
            nc.tensor.transpose(side_bank[:, quarters[place]], prob[0][:, quarters[q]], ident[:])
        side = sb.tile([P, len(joined_quarters) * P + GATE_COLUMNS], F32, name="side")
        nc.scalar.copy(side[:], side_bank[:, : len(joined_quarters) * P + GATE_COLUMNS])
        gate_columns = side[:, len(joined_quarters) * P :]
        sum_half0 = ps.tile([P, S // 2], F32, name="sum_half0", tag="bank6")
        sum_quarter3 = ps.tile([P, P], F32, name="sum_quarter3", tag="bank4")
        for q in range(2):
            nc.tensor.matmul(sum_half0[:, quarters[q]], side[:, quarters[q]], ident[:], is_transpose=True, start=(q == 0), stop=False)
        nc.tensor.matmul(sum_quarter3[:], side[:, quarters[2]], ident[:], is_transpose=True, start=True, stop=False)

        weighed = [[sb.tile([P, P], F32, name=f"weighed{d}{q}", tag=f"weighed{d}{q}") for q in range(len(quarters))] for d in range(2)]

        def fetch_and_turn(d, cols, tag, buffer):
            fetched = sb.tile([P, cols.stop - cols.start], F32, name=f"fetched{d}_{cols.start}", tag=buffer)
            nc.scalar.activation(fetched[:], errors[0][:].indirect(pos_t[d][:, entries(cols)]), ACT.Copy)
            bank = ps.tile([P, cols.stop - cols.start], F32, name=f"turned{d}_{cols.start}", tag=tag)
            for c in range(cols.start, cols.stop, P):
                nc.tensor.transpose(bank[:, c - cols.start : c - cols.start + P], fetched[:, c - cols.start : c - cols.start + P], ident[:])
            return bank

        def weigh_turned(d, cols, bank):
            for c in range(cols.start, cols.stop, P):
                column = len(quarters) * d + c // P
                nc.scalar.activation(
                    weighed[d][c // P][:], bank[:, c - cols.start : c - cols.start + P], ACT.Copy, scale=gate_columns[:, column : column + 1]
                )

        term = [sb.tile([P, S], F32, name=f"term{d}", tag=f"term{d}") for d in range(2)]
        part = sb.tile([P, S], F32, name="part")

        def fetch(d, cols):
            nc.vector.tensor_tensor(term[d][:, cols], errors[1][:].indirect(pos_t[d][:, entries(cols)]), gate_t[d][:, cols], ALU.mult)

        def add_first(cols):
            nc.vector.tensor_tensor(part[:, cols], term[0][:, cols], prob[1][:, cols], ALU.add)

        def add_second(cols):
            nc.vector.tensor_tensor(result1[:, cols], part[:, cols], term[1][:, cols], ALU.add)
            nc.sync.dma_start(out[panels[1], cols], result1[:, cols])

        list0_half0 = fetch_and_turn(0, halves[0], "bank0", "fetched00")
        list1_half0 = fetch_and_turn(1, halves[0], "bank1", "fetched10")
        list1_half1 = fetch_and_turn(1, halves[1], "bank2", "fetched01")
        weigh_turned(0, halves[0], list0_half0)
        weigh_turned(1, halves[0], list1_half0)
        for d in range(2):
            for q in range(2):
                nc.tensor.matmul(sum_half0[:, quarters[q]], weighed[d][q][:], ident[:], is_transpose=True, start=False, stop=(d == 1 and q == 1))
        list0_quarter2 = fetch_and_turn(0, quarters[2], "bank5", "fetched11")
        weigh_turned(1, halves[1], list1_half1)
        weigh_turned(0, quarters[2], list0_quarter2)
        nc.tensor.matmul(sum_quarter3[:], weighed[1][3][:], ident[:], is_transpose=True, start=False, stop=True)
        sum_quarter2 = ps.tile([P, P], F32, name="sum_quarter2", tag="bank3")
        for d in (1, 0):
            nc.tensor.matmul(sum_quarter2[:], weighed[d][2][:], ident[:], is_transpose=True, start=(d == 1), stop=(d == 0))
        result0_half0 = sb.tile([P, S // 2], F32, name="result0_half0", tag="fetched11")
        nc.scalar.copy(result0_half0[:], sum_half0[:])
        nc.scalar.dma_start(out[panels[0], halves[0]], result0_half0[:])

        def finish_quarter(q, missing, bank):
            nc.vector.tensor_tensor(result0[:, quarters[q]], missing, bank[:], ALU.add)
            nc.sync.dma_start(out[panels[0], quarters[q]], result0[:, quarters[q]])

        fetch(0, slice(0, S))
        fetch(1, halves[0])
        add_first(halves[0])
        add_first(halves[1])
        result0 = sb.tile([P, S], F32, name="result0", tag="term0")
        add_second(halves[0])
        fetch(1, halves[1])
        finish_quarter(3, corner[:], sum_quarter3)
        add_second(halves[1])
        finish_quarter(2, prob[0][:, quarters[2]], sum_quarter2)
